import numpy as np, ml_dtypes
CORES = [83,85,87,115,117,119]
N = 6
BF = ml_dtypes.bfloat16
W, K, T, S, ND = 4096, 384, 3, 5, 2
def stir(rng, a, n):
    r = rng.random(a.shape, dtype=np.float32)
    s = np.concatenate([np.sort(r, axis=-1), np.full(r.shape[:-1] + (1,), 2, np.float32)], axis=-1)
    return np.where(r < np.take_along_axis(s, n[..., None], -1), (a + rng.integers(1, 64, a.shape)) & 63, a)
def near(rng, pro, n, counts):
    a = pro[np.arange(8)[None, :, None], rng.integers(0, pro.shape[1], (N, 8, n))]
    return stir(rng, a, rng.choice(np.array(counts), (N, 8, n)))
def protos(rng, first):
    return stir(rng, np.repeat(first, 2, axis=1), np.full((8, 2), 3))
def parts(rng):
    pro = protos(rng, rng.integers(0, 64, (8, 1, 16)))
    return (near(rng, pro, K, [0, 1, 1, 2, 2, 3, 16]), rng.integers(0, 256, (N, 8, K, 16)), near(rng, pro, W, [0, 1, 1, 2, 3, 16]), rng.integers(0, 256, (N, 8, W, 16)),
            rng.integers(0, 256, (8, 16, 2)), rng.integers(900, 1900, (N, 8, 16)))
def tile(a):
    return np.ascontiguousarray(a.transpose(0, 1, 3, 2)).reshape(N, 128, -1).astype(np.float32).astype(BF)
def pack(x, g, lx, lm, w, lim):
    return {"xw": tile(x), "gw": tile(g), "lex": tile(lx), "mng": tile(lm),
            "wts": np.ascontiguousarray(np.broadcast_to(w.reshape(1, 128, 2), (N, 128, 2))).astype(np.int32), "th": lim.reshape(N, 128, 1).astype(np.int32)}
def setup_inputs(rng):
    return pack(*parts(rng))
def setup_inputs_spread(rng):
    pro = protos(rng, (64 * rng.random((8, 1, 16)) ** 3).astype(np.int64))
    x = near(rng, pro, K, [0, 1, 1, 2, 3, 4, 16]); lx = near(rng, pro, W, [0, 1, 1, 2, 4, 16])
    g = np.floor(256 * rng.random((N, 8, K, 1)) ** 2 * rng.random((N, 8, K, 16))).astype(np.int64)
    lm = np.floor(256 * rng.random((N, 8, W, 1)) ** 2 * rng.random((N, 8, W, 16))).astype(np.int64)
    w = np.exp2(8 * rng.random((8, 16, 2))).astype(np.int64) - 1; w = np.where(rng.random(w.shape) < 0.25, rng.integers(0, 256, w.shape), w)
    lim = np.minimum(np.exp2(4 + 8.2 * rng.random((N, 8, 16))).astype(np.int64), 4081)
    return pack(x, g, lx, lm, w, lim)
def setup_inputs_ends(rng):
    base = np.repeat(63 * rng.integers(0, 2, (8, 1, 16)), 2, axis=1); base[:, 1] = np.where(rng.random((8, 16)) < 0.15, 63 - base[:, 1], base[:, 1])
    def some(n, share):
        a = base[np.arange(8)[None, :, None], rng.integers(0, 2, (N, 8, n))]
        return np.where(rng.random(a.shape) < share, np.where(rng.random(a.shape) < 0.6, 63 - a, rng.choice(np.array([1, 31, 62]), a.shape)), a)
    def both(n):
        return 255 * np.where(rng.random((N, 8, n, 1)) < 0.5, rng.integers(0, 2, (N, 8, n, 1)), rng.integers(0, 2, (N, 8, n, 16)))
    x = some(K, 0.08); lx = some(W, 0.1); g = both(K); lm = both(W)
    w = 255 * rng.integers(0, 2, (8, 16, 2)); w[:5, 15] = 65; w[5, :, 0] = 255; w[6, 0] = 65; w[7, 14:, 0] = 65; w[7, 14:, 1] = 0
    w[4, 13, 0] = 89; w[4, 13, 1] = 0; w[4, 14, 0] = 0; w[4, 14, 1] = 227
    lim = np.full((N, 8, 16), 4081); odd = np.arange(N) % 2 == 1
    lim = np.where(odd[:, None, None] & (rng.random(lim.shape) < 0.25), 0, lim); lim[:, 0, 0] = 0
    x[:, 0, :, 0] = 63; lx[:, 0, :, 0] = 63
    x[:, 5, 1] = 63; x[:, 5, K - 1] = 63
    for i in (3, K - 2):
        x[:, 1:5, i] = 0; x[:, 1:5, i, 15] = 63
    p = (((W - 1) ** 2 >> 5) + W - 1) & (W - 1)
    lx[:, 1:5, p] = 0; lx[:, 1:5, p, 15] = 63; lx[:, 1:5, p, 13] = 63
    x[:, 4, 4] = 0; x[:, 4, 4, 13] = 46; x[:, 4, 4, 14] = 36; x[:, 4, 4, 15] = 63
    p = ((4093 * 4075 >> 5) + 4093) & (W - 1)
    lx[:, 4, p] = x[:, 4, 4]; lx[:, 4, p, 0] = 63; lx[:, 4, p + 1] = 63; lm[:, 4, p] = 255; g[:, 4, 4] = 0
    x[:, 7, 4] = 0; x[:, 7, 4, 14] = 63; g[:, 7, 4] = 0
    for i in (5, K - 1):
        x[:, 7, i] = 0; x[:, 7, i, 15] = 63; g[:, 7, i] = 255 if i == 5 else 0
    lx[:, 7, 0] = 63; lx[:, 7, W - 1] = 0; lx[:, 7, W - 1, 14:] = 63; lm[:, 7, W - 1] = 255
    g[:, 6, :, 15] = 255; lm[:, 6, :, 15] = 255; g[:, 6, :, 14] = 0; lm[:, 6, :, 14] = 0
    return pack(x, g, lx, lm, w, lim)
def setup_inputs_corners(rng):
    pro = rng.integers(0, 64, (8, 1, 16)); lx = near(rng, pro, W, [0, 0, 1]); lx[:, :, 0] = pro[:, 0]
    x = near(rng, pro, K, [0, 1, ND, ND + 1, ND + 2, 16])
    w = rng.integers(0, 256, (8, 16, 2)); w[0] = 0; w[1] = 255; w[2, :, 0] = 0; w[2, :, 1] = 255; w[3, :, 1] = w[3, :, 0]; w[4, :15] = 0; w[4, 15] = 255; w[5, 1:] = 0; w[5, 0] = 255
    w[6] = 255 * rng.integers(0, 2, (16, 2)); w = w[rng.permutation(8)]
    def mean(n):
        return np.where(rng.random((N, 8, n, 1)) < 0.6, 255 * rng.integers(0, 2, (N, 8, n, 1)), rng.integers(0, 256, (N, 8, n, 16)))
    case = (np.arange(8)[None, :] + np.arange(N)[:, None] + rng.integers(0, 5)) % 5; case = case[:, :, None]
    lim = np.where(case == 0, 0, np.where(case == 1, 4081, np.where(case == 2, 4081 * rng.integers(0, 2, (N, 8, 16)), np.where(case == 3, 1, rng.integers(900, 1900, (N, 8, 16))))))
    return pack(x, mean(K), lx, mean(W), w, lim)
def setup_inputs_ties(rng):
    pro = rng.integers(0, 64, (8, 1, 16)); far = np.where(rng.permutation(8) < 4, 0, rng.integers(130, 251, 8)).reshape(8, 1, 1)
    b = rng.integers(0, 255 - far, (8, 1, 16)); side = rng.integers(0, 2, (8, 1, 16))
    x = near(rng, pro, K, [0, 1, 1, 1]); lx = near(rng, pro, W, [0, ND, ND, ND + 1])
    g = b + far * side + rng.integers(0, 2, (N, 8, K, 16)); lm = b + far * (1 - side) + rng.integers(0, 2, (N, 8, W, 16))
    lim = np.where(far[:, 0] == 0, rng.integers(5, 13, (N, 8, 16)), 16 * far[:, 0] + rng.integers(-3, 5, (N, 8, 16)))
    return pack(x, g, lx, lm, rng.integers(0, 256, (8, 16, 2)), lim)
def setup_inputs_alike(rng):
    o = rng.permutation(64); al = o[:4]; kinds = (rng.integers(0, 4, (8, 1, 16)) + (rng.random((8, 6, 16)) < 0.12) * rng.integers(1, 4, (8, 6, 16))) & 3
    pro = al[kinds]; x = near(rng, pro, K, [0]); lx = near(rng, pro, W, [0])
    g = rng.integers(0, 256, (N, 8, K, 16)); lm = rng.integers(0, 256, (N, 8, W, 16)); w = rng.integers(0, 256, (8, 16, 2))
    even = (np.arange(N) % 2 == 0)[:, None, None]
    lim = np.where((rng.random((N, 8, 1)) < 0.6) | even, 4081, rng.integers(900, 1900, (N, 8, 16)))
    two = np.sort(o[4:12].reshape(4, 2), axis=1); spot = np.arange(W); four = [int(e) for e in rng.permutation(8)[:4]]
    for e in four:
        lx[:, e] = pro[e, 0]; lx[:, e, :, 0] = two[spot & 3, 1]; lx[:, e, :, 14] = spot & 63; lx[:, e, :, 15] = spot >> 6
        w[e] = 0; w[e, 14, 0] = 1; w[e, 15, 0] = 64; lim[:, e] = 4081
    for r in range(N):
        j = rng.permutation(W >> 1)[:K]
        put = [4 * (j >> 1) + 2 + (j & 1),
               np.full(K, 4 * rng.integers(0, W >> 2) + 2 + rng.integers(0, 2)),
               4 * rng.permutation(W >> 2)[:K] + (np.arange(K) >= 256),
               np.repeat(4 * rng.permutation(W >> 2)[:K >> 1] + (np.arange(K >> 1) & 3), 2)]
        for e, p in zip(four, put):
            x[r, e] = pro[e, 0]; x[r, e, :, 0] = two[p & 3, 0]; x[r, e, :, 14] = p & 63; x[r, e, :, 15] = p >> 6
    e = four[2]
    g[:, e] = rng.integers(0, 41, (N, K, 16)) + 200 * even; lm[:, e] = rng.integers(0, 41, (N, W, 16)); lim[:, e] = rng.integers(700, 2500, (N, 16))
    return pack(x, g, lx, lm, w, lim)
def check_inputs(d):
    bad = []
    for k, lo, hi in (("xw", 0, 63), ("gw", 0, 255), ("lex", 0, 63), ("mng", 0, 255), ("wts", 0, 255), ("th", 0, 4081)):
        a = np.asarray(d[k]).astype(np.float64)
        if not (np.min(a) >= lo and np.max(a) <= hi): bad.append("range of " + k)
        elif np.any(a != np.floor(a)): bad.append("whole numbers of " + k)
    a = np.asarray(d["wts"])
    if np.any(a != a[:1]): bad.append("wts alike on all ranks")
    return bad
def visit(t, x, g, lx, lm, w, lim):
    p = w[..., :1] * x; u = (np.add.reduce(p, axis=1, keepdims=True) - p) & (W - 1)
    p = w[..., 1:] * x; u2 = (np.add.reduce(p, axis=1, keepdims=True) - p) & (W - 1)
    h = (((u * u2) >> 5) + u) & (W - 1)
    c = np.take_along_axis(lx, h.reshape(8, 1, 16 * K), 2).reshape(8, 16, 16, K)
    m = np.take_along_axis(lm, h.reshape(8, 1, 16 * K), 2).reshape(8, 16, 16, K)
    differ = np.add.reduce((c != x[:, :, None, :]).astype(np.int32), axis=1)
    far = np.add.reduce(np.abs(m - g[:, :, None, :]), axis=1)
    lane = np.arange(16); b = c[:, lane, lane, :]
    pair = (b != x) & (differ <= ND + 1)
    has = np.any(pair, axis=1); f = np.argmax(pair, axis=1)[:, None, :]
    def at(a):
        return np.take_along_axis(a, f, 1)[:, 0]
    xa, xb, hf = at(x), at(b), at(h)
    free = at((far < lim).astype(np.int32)) == 1
    pc = 64 * np.minimum(xa, xb) + np.maximum(xa, xb)
    flag = np.zeros(4096, bool); flag[pc[has & ~free]] = True
    merge = has & free & ~flag[pc]
    mf = np.take_along_axis(lm, hf[:, None, :], 2)
    row = lane[None, :, None]
    xn = np.where((row == f) & merge[:, None, :], np.minimum(x, b), x)
    xn = np.where((row == t) & ~has[:, None, :], b, xn)
    gn = np.where(merge[:, None, :], (g + mf) >> 1, g)
    for e in range(8):
        for i in np.flatnonzero(merge[e])[::-1]:
            lx[e, :, hf[e, i]] = xn[e, :, i]; lm[e, :, hf[e, i]] = gn[e, :, i]
    x[...] = xn; g[...] = gn
def reference(xw, gw, lex, mng, wts, th):
    x = xw.astype(np.float32).astype(np.int32).reshape(N, 8, 16, K); g = gw.astype(np.float32).astype(np.int32).reshape(N, 8, 16, K)
    lx = lex.astype(np.float32).astype(np.int32).reshape(N, 8, 16, W); lm = mng.astype(np.float32).astype(np.int32).reshape(N, 8, 16, W)
    w = wts.astype(np.int32).reshape(N, 8, 16, 2); lim = th.astype(np.int32).reshape(N, 8, 16, 1)
    for t in range(T):
        for r in range(N):
            v = (r + S * t) % N; visit(t, x[r], g[r], lx[v], lm[v], w[v], lim[v])
    return {"yx": x.reshape(N, 128, K).astype(np.float32).astype(BF), "yg": g.reshape(N, 128, K).astype(np.float32).astype(BF),
            "yl": lx.reshape(N, 128, W).astype(np.float32).astype(BF), "ym": np.add.reduce(lm, axis=3).reshape(N, 128, 1).astype(np.float32)}

@@ -1,0 +1,481 @@
+from concourse.mybir import dt, AluOpType, AxisListType, ActivationFunctionType
+
+N, W, K, VIS = 6, 4096, 384, 3
+HBL = [(0, 128), (128, 384)]
+BLK = [(0, 128), (128, 256), (256, 320), (320, 384)]
+NENG = 8
+BF, F32, I32, U16, F16 = "bfloat16", "float32", "int32", "uint16", "float16"
+SCRATCH = {
+    "lx": ("sbuf", [128, W + K], BF), "mn": ("sbuf", [128, W + K], BF),
+    "wti": ("sbuf", [128, 2], I32), "thi": ("sbuf", [128, 1], I32), "pi": ("sbuf", [128, 1], I32), "pj": ("sbuf", [128, 4], I32),
+    "col": ("sbuf", [128, 24], F32), "i64": ("sbuf", [128, 64], BF), "one": ("sbuf", [128, 256], BF), "neg": ("sbuf", [128, 64], BF), "C": ("sbuf", [128, 1024], BF), "CA": ("sbuf", [128, 1024], BF), "la": ("sbuf", [128, K], BF),
+    "X16": ("sbuf", [128, 16 * K], BF), "D": ("sbuf", [128, 16 * K], BF), "E": ("sbuf", [128, 24 * K], BF), "UP": ("sbuf", [128, 256], F32), "Mh": ("sbuf", [128, 512], BF),
+    "hi": ("sbuf", [128, K], I32), "hu": ("sbuf", [128, K], U16), "hd": ("sbuf", [128, K], I32), "Lh": ("sbuf", [128, K], F16), "Hb": ("sbuf", [128, K], F16),
+    "le": ("sbuf", [128, 24], U16), "lf": ("sbuf", [128, 24], U16), "lo": ("sbuf", [128, 24], U16),
+    "ab": ("sbuf", [128, 1536], BF), "U": ("sbuf", [128, 1536], BF), "TS": ("sbuf", [128, 64], BF), "TW": ("sbuf", [128, 256], BF),
+    "ya": ("sbuf", [128, 1], F32), "yb": ("sbuf", [128, 1], F32), "ys": ("sbuf", [128, 1], F32),
+}
+for _n in ("x0 x1 x2 x3 m0 m1 m2 m3 xn0 xn1 xn2 gn0 gn1 gn2 pm Le Fm nb NP Lx d ad LC LCm XB XC lh RF tx M nM gd LB").split():
+    SCRATCH[_n] = ("sbuf", [128, K], BF)
+for _n in ("cg cl cq B Id BmI up L Lm Gm Wv0 Wv1 Wv2 Wa Wb C6 NI4 MI NI16 I14 FLM FAm FBm").split():
+    SCRATCH[_n] = ("sbuf", [128, 128], BF)
+for _n in ("B8 PH MH WFA WFB").split():
+    SCRATCH[_n] = ("sbuf", [128, 8], BF)
+for _n in ("wr3 WR WI WG CK CN").split():
+    SCRATCH[_n] = ("sbuf", [128, 2048], BF)
+for _n in ("sbi SEL").split():
+    SCRATCH[_n] = ("sbuf", [128, 512], BF)
+for _n in ("pr ps pt").split():
+    SCRATCH[_n] = ("sbuf", [128, 256], I32)
+for _n in ("eq cw ge").split():
+    SCRATCH[_n] = ("sbuf", [128, 16], F32)
+for _n in ("ci cim mc rc nf hw hp z z1 z2 z3").split():
+    SCRATCH[_n] = ("sbuf", [128, 24], F32)
+for _b in range(8):
+    SCRATCH["b%d" % _b] = ("psum", [128, 512], F32)
+SEMAPHORES = ["qv", "qs", "qt", "qg", "lx", "lw", "lt", "lg", "ll", "lm", "ax1", "ag1", "ax2", "ag2", "ax3", "ag3", "rl", "ox", "og", "ol", "om"]
+
+
+def rank_program(g, core, T, topo):
+    rank = T.rank_of(core)
+    if rank is None:
+        return
+    A, AF = AluOpType, ActivationFunctionType
+    Q = {"v": g.vector, "s": g.scalar, "t": g.tensor, "g": g, "y": g.sync}
+    own = {"v": "qv", "s": "qs", "t": "qt", "g": "qg"}
+    cnt = {"v": 0, "s": 0, "t": 0, "g": 0}
+    known = {q: {} for q in Q}
+    past = {}
+    acc = {}
+
+    def ref(name, lo=0, hi=None, step=1, p=128):
+        hi = T[name].shape[1] if hi is None else hi
+        return (name, lo, hi, T[name][0:p, lo:hi:step] if step != 1 else T[name][0:p, lo:hi])
+
+    def is_ps(name):
+        return name in SCRATCH and SCRATCH[name][0] == "psum"
+
+    def need(q, reads, writes):
+        me = own.get(q)
+        dep = {}
+        for rs, w in ((reads, False), (writes, True)):
+            for (name, lo, hi, _) in rs:
+                for (l2, h2, ev, c, w2) in acc.get(name, []):
+                    if is_ps(name):
+                        hit = ev != me or (q != "t" and (w or w2) and l2 < hi and lo < h2)
+                    else:
+                        hit = l2 < hi and lo < h2 and (w or w2)
+                    if hit and dep.get(ev, 0) < c:
+                        dep[ev] = c
+        todo = {e: c for e, c in dep.items() if known[q].get(e, 0) < c}
+        for e in list(todo):
+            if any(f != e and past.get((f, todo[f]), {}).get(e, 0) >= todo[e] for f in todo):
+                del todo[e]
+        for e, c in todo.items():
+            Q[q].wait_ge(T.sem[e], c)
+            k = known[q]
+            k[e] = max(k.get(e, 0), c)
+            for e2, c2 in past.get((e, c), {}).items():
+                k[e2] = max(k.get(e2, 0), c2)
+
+    def note(ev, c, q, reads, writes):
+        k = dict(known[q]) if q else {}
+        k[ev] = c
+        past[(ev, c)] = k
+        for rs, w in ((reads, False), (writes, True)):
+            for (name, lo, hi, _) in rs:
+                old = acc.get(name, [])
+                if w:
+                    old = [o for o in old if not (lo <= o[0] and o[1] <= hi) or (is_ps(name) and o[2] != ev)]
+                else:
+                    old = [o for o in old if not (o[2] == ev and not o[4] and lo <= o[0] and o[1] <= hi)]
+                acc[name] = old + [(lo, hi, ev, c, w)]
+
+    def do(q, fn, reads, writes):
+        need(q, reads, writes)
+        ins = fn()
+        cnt[q] += 1
+        ins.then_inc(T.sem[own[q]], 1)
+        note(own[q], cnt[q], q, reads, writes)
+
+    def rd(*xs):
+        out = []
+        for x in xs:
+            if isinstance(x, tuple):
+                out += x[1] if x[0] is None else [x]
+        return out
+
+    def ap(x):
+        return x[-1] if isinstance(x, tuple) else x
+
+    def ind(win, off):
+        return (None, [win, off], win[3].indirect(off[3]))
+
+    def tt(out, a, b, op):
+        do("v", lambda: g.vector.tensor_tensor(ap(out), ap(a), ap(b), op), rd(a, b), rd(out))
+
+    def ts(out, a, s1, op0, s2=None, op1=None):
+        if op1 is None:
+            do("v", lambda: g.vector.tensor_scalar(ap(out), ap(a), ap(s1), None, op0), rd(a, s1), rd(out))
+        else:
+            do("v", lambda: g.vector.tensor_scalar(ap(out), ap(a), ap(s1), ap(s2), op0, op1), rd(a, s1, s2), rd(out))
+
+    def cp(out, a):
+        do("v", lambda: g.vector.tensor_copy(ap(out), ap(a)), rd(a), rd(out))
+
+    def fill(out, c):
+        do("v", lambda: g.vector.memset(ap(out), c), [], rd(out))
+
+    def act(out, a, f, bias=0.0, scale=1.0, accum=None):
+        if accum is None:
+            do("s", lambda: g.scalar.activation(ap(out), ap(a), f, bias=ap(bias), scale=ap(scale)), rd(a, bias, scale), rd(out))
+        else:
+            do("s", lambda: g.scalar.activation(ap(out), ap(a), f, bias=ap(bias), scale=ap(scale), accum_out=ap(accum)), rd(a, bias, scale), rd(out, accum))
+
+    def mm(out, l, r, start, stop):
+        do("t", lambda: g.tensor.matmul(ap(out), ap(l), ap(r), start, stop), rd(l, r), rd(out))
+
+    def iota(out, pattern, base, cm, small=True):
+        if small:
+            do("g", lambda: g.iota(ap(out), pattern, base, cm, allow_small_or_imprecise_dtypes=True), [], rd(out))
+        else:
+            do("g", lambda: g.iota(ap(out), pattern, base, cm), [], rd(out))
+
+    def load(q, out, src, sem):
+        Q[q].dma_start(ap(out), src).then_inc(T.sem[sem], 16)
+        note(sem, 16, None, [], rd(out))
+
+    def store(q, dst, src, sem):
+        need(q, rd(src), [])
+        Q[q].dma_start(dst, ap(src)).then_inc(T.sem[sem], 16)
+        note(sem, 16, q, rd(src), [])
+
+    sent = [0]
+
+    def send(src, dst, to, sem):
+        c = T.cores[to]
+        m = 0
+        for e in topo.engines(core, c)[:NENG]:
+            m |= 1 << e
+        rid, pid, _ = topo.addr(c)
+        need("g", rd(src), [])
+        g.remote_dma(ap(dst), ap(src), T.sem[sem], T.sem["rl"], pid, rid, m)
+        sent[0] += NENG
+
+    load("y", ref("x0"), T.xw[:, :], "lx")
+    load("y", ref("wti"), T.wts[:, :], "lw")
+    load("s", ref("lx", 0, W), T.lex[:, :], "ll")
+    load("y", ref("m0"), T.gw[:, :], "lg")
+    load("y", ref("thi"), T.th[:, :], "lt")
+    load("s", ref("mn", 0, W), T.mng[:, :], "lm")
+    for t in (1, 2, 3):
+        note("ax%d" % t, NENG, None, [], [ref("x%d" % t)])
+        note("ag%d" % t, NENG, None, [], [ref("m%d" % t)])
+
+    iota(ref("pi"), [[1, 1]], 0, 1, False)
+    iota(ref("cq"), [[1, 128]], 0, 0)
+    iota(ref("cg"), [[1, 8], [0, 16]], 0, 0)
+    iota(ref("cl"), [[0, 8], [1, 16]], 0, 0)
+    iota(ref("i64"), [[1, 64]], 0, 0)
+    iota(ref("ci"), [[16, 24]], 2048, 0)
+    iota(ref("wr3"), [[-100, 16], [1, 8], [100, 16]], 0, 0)
+    iota(ref("sbi"), [[16, 4], [0, 8], [1, 16]], 0, 0)
+
+    def col(j):
+        return ref("col", j, j + 1)
+    PG, PL, PP, PLM, THR, W1, W2, THA, THB, C_FAM, C_FBM, C_WA = 0, 1, 2, 3, 4, 7, 8, 9, 10, 11, 12, 13
+    B, Id = ref("B"), ref("Id")
+    ts(ref("pj", 0, 1), ref("pi"), 4, A.arith_shift_right)
+    ts(ref("pj", 1, 2), ref("pi"), 15, A.bitwise_and)
+    fill(ref("C6"), 6144.0)
+    fill(ref("one"), 1.0)
+    fill(ref("neg"), -1.0 / 128)
+    cp(col(PG), ref("pj", 0, 1))
+    cp(col(PL), ref("pj", 1, 2))
+    cp(col(PP), ref("pi"))
+    ts(Id, ref("cq"), col(PP), A.is_equal)
+    ts(B, ref("cg"), col(PG), A.is_equal)
+    act(ref("NI4"), Id, AF.Copy, scale=-4096.0)
+    tt(ref("BmI"), B, Id, A.subtract)
+    ts(ref("eq"), ref("cl", 0, 16), col(PL), A.is_equal)
+    fill(ref("CK"), 0.0)
+    ts(ref("cw"), ref("eq"), -17.0, A.mult, 1.0, A.add)
+    cp(ref("B8"), ref("B", 0, 128, 16))
+    cp(ref("col", W1, W1 + 2), ref("wti"))
+    ts(ref("Wa"), ref("BmI"), col(W1), A.mult)
+    ts(ref("Wb"), ref("BmI"), col(W2), A.mult)
+    for k in range(16):
+        ts(ref("CK", 129 * k, 128 * k + 128, 16), ref("B8"), ref("cw", k, k + 1), A.mult)
+
+    def more_constants():
+        for name, src, s in (("MI", "Id", -1.0), ("NI16", "Id", -16.0),
+                             ("I14", "Id", 2.0 ** -14), ("FLM", "B", 4096.0), ("PH", "B8", 0.5), ("MH", "B8", -0.5)):
+            act(ref(name), ref(src), AF.Copy, scale=s)
+        act(ref("CN"), ref("CK"), AF.Copy, scale=-1.0)
+
+    def picks(mat, scale):
+        act(ref(mat), ref("wr3"), AF.Copy, scale=0.0)
+        for r in range(16):
+            act(ref(mat, 129 * r, 128 * r + 128, 16), ref("B8"), AF.Copy, scale=ref(scale, r, r + 1))
+
+    def v_constants():
+        ts(ref("up"), ref("cl"), col(PL), A.is_gt)
+        tt(ref("L"), ref("up"), B, A.mult)
+        ts(ref("Lm"), ref("L"), -128.0, A.mult)
+        tt(ref("Gm"), ref("BmI"), ref("L"), A.subtract)
+        ts(ref("Gm"), ref("Gm"), 2.0 ** -14, A.mult)
+        for t in range(VIS):
+            w = "Wv%d" % t
+            tt(ref(w), ref("Lm"), Id, A.add)
+            tt(ref(w, t, 128, 16), ref(w, t, 128, 16), ref("Gm", t, 128, 16), A.subtract)
+            ts(col(THR + t), col(PL), float(t), A.not_equal)
+        ts(ref("WR"), ref("wr3"), col(PG), A.is_equal)
+        ts(ref("pj", 2, 3), ref("thi"), 4, A.arith_shift_right)
+        ts(ref("pj", 3, 4), ref("thi"), 15, A.bitwise_and)
+        cp(ref("col", THA, THA + 2), ref("pj", 2, 4))
+        ts(col(C_FAM), col(THA), -16.0, A.mult)
+        ts(col(C_FBM), col(THB), -1.0, A.mult)
+        ts(col(C_WA), col(THA), -16.0, A.mult, 4096.0, A.add)
+        for name, src, c in (("FAm", "B", C_FAM), ("FBm", "B", C_FBM), ("WFA", "B8", C_WA), ("WFB", "B8", C_FBM)):
+            ts(ref(name), ref(src), col(c), A.mult)
+        ts(ref("SEL", p=64), ref("sbi", p=64), ref("col", PP, PP + 1, p=64), A.is_equal)
+        ts(ref("cim"), ref("ci"), col(PL), A.add)
+        ts(col(PLM), col(PL), -1.0, A.mult, 3072.0, A.add)
+        ts(ref("ge"), ref("cl", 0, 16), col(PL), A.is_le, 65536.0, A.mult)
+
+    def full(b, n=K):
+        return ref("b%d" % b, 0, n)
+
+    def wrap(out, mat, src, first, last):
+        for r in range(16):
+            mm(out, ref(mat, 128 * r, 128 * r + 128), ref(src, r, K, 16), first and r == 0, last and r == 15)
+
+    lexw, mngw = ref("lx", 0, W), ref("mn", 0, W)
+
+    def spread(t, b, on_v):
+        i0, i1 = BLK[b]
+        for k in range(16):
+            o, s = ref("X16", 16 * i0 + k, 16 * i1, 16), ref("x%d" % t, i0, i1)
+            if on_v:
+                cp(o, s)
+            else:
+                act(o, s, AF.Copy)
+
+    def hash_s(t, b):
+        hash_1(t, b)
+        hash_2(b)
+        hash_3(b)
+
+    def hash_1(t, b):
+        i0, i1 = HBL[b]
+        n = i1 - i0
+        xs = ref("x%d" % t, i0, i1)
+        mm(ref("b0", 0, n), ref("Wa"), xs, True, True)
+        mm(ref("b0", n, 2 * n), ref("Wb"), xs, True, True)
+        mm(full(2, n), ref("Wb"), xs, True, False)
+        mm(full(1, n), ref("C6"), ref("one", 0, n), True, False)
+        mm(full(1, n), ref("Wa"), xs, False, False)
+
+    def hash_2(b):
+        n = HBL[b][1] - HBL[b][0]
+        act(ref("Mh", 0, 2 * n), ref("b0", 0, 2 * n), AF.Identity, bias=192.0 - 4095.0 / 8192.0, scale=1.0 / 4096.0)
+
+    def hash_3(b):
+        n = HBL[b][1] - HBL[b][0]
+        mm(full(2, n), ref("NI4"), ref("Mh", n, 2 * n), False, True)
+        mm(full(1, n), ref("NI4"), ref("Mh", 0, n), False, True)
+        act(ref("UP", 0, n), full(2, n), AF.Identity, bias=786432.0)
+
+    def hash_v(b):
+        i0, i1 = HBL[b]
+        n = i1 - i0
+        tt(ref("pr", 0, n), ref("UP", 0, n), full(1, n), A.mult)
+        ts(ref("ps", 0, n), ref("pr", 0, n), 5, A.arith_shift_right)
+        tt(ref("pt", 0, n), ref("ps", 0, n), full(1, n), A.add)
+        ts(ref("hi", i0, i1), ref("pt", 0, n), 4095, A.bitwise_and)
+        cp(ref("hu", i0, i1), ref("hi", i0, i1))
+
+    def look(b):
+        i0, i1 = BLK[b]
+        dd = ref("D", 16 * i0, 16 * i1)
+        tt(dd, ind(lexw, ref("hu", i0, i1)), ref("X16", 16 * i0, 16 * i1), A.not_equal)
+        for k in range(16):
+            mm(ref("b3", i0, i1), ref("CK", 128 * k, 128 * k + 128), ref("D", 16 * i0 + k, 16 * i1, 16), k == 0, k == 15)
+
+    def look_s(t, b):
+        i0, i1 = BLK[b]
+        n = i1 - i0
+        w, o = lexw, ref("hu", i0, i1)
+        do("s", lambda: g.scalar.activation(ref("C")[3], w[3].indirect(o[3]), AF.Copy), [w, o], [ref("C")])
+        for h in range(2):
+            for k in range(8):
+                c = ref("b%d" % (6 + h), n * k, n * k + n)
+                mm(c, ref("MI"), ref("x%d" % t, i0, i1), True, False)
+                mm(c, Id, ref("C", 8 * h + k, 1024, 16), False, True)
+        for h in range(2):
+            act(ref("CA", 512 * h, 512 * h + 512), full(6 + h, 512), AF.Abs)
+        act(ref("C"), ref("CA"), AF.Relu, bias=1.0, scale=-1.0)
+
+    def count_s(b):
+        i0, i1 = BLK[b]
+        n = i1 - i0
+        mm(ref("b3", i0, i1), ref("one", 0, 128), ref("neg", 0, n), True, False)
+        for h in range(2):
+            for k in range(8):
+                j = 8 * h + k
+                mm(ref("b3", i0, i1), ref("CN", 128 * j, 128 * j + 128), ref("C", n * j, n * j + n), False, j == 15)
+
+    def scatter(buf, src):
+        w, o, s = ref(buf), ref("lo"), ref(src)
+        do("v", lambda: g.vector.tensor_copy(w[3].indirect(o[3]), s[3]), [o, s], [w])
+
+    hash_s(0, 0)
+    spread(0, 0, True)
+    hash_v(0)
+    for t in range(VIS):
+        x, m, last = "x%d" % t, "m%d" % t, t == VIS - 1
+        xn, gn = "xn%d" % t, "gn%d" % t
+        to = (rank + 2) % N if last else (rank - 1) % N
+
+        hash_s(t, 1)
+        look(0)
+        spread(t, 1, False)
+        if t == 0:
+            more_constants()
+        hash_v(1)
+        spread(t, 2, False)
+        look_s(t, 3)
+        act(full(4), ref(x), AF.Copy)
+        look(1)
+        count_s(3)
+        look(2)
+        if t == 0:
+            v_constants()
+            picks("WI", "eq")
+        ts(full(5), ref("hi"), -2048.0, A.add)
+        if t > 0:
+            scatter("mn", "gn%d" % (t - 1))
+
+        ts(ref("pm"), full(3), -13.5, A.is_le)
+        mm(full(0), ref("Wv%d" % t), ref("pm"), True, True)
+        ts(ref("Le"), full(0), col(THR + t), A.is_ge)
+        act(ref("Fm"), full(0), AF.Relu)
+        act(ref("nb"), full(0), AF.Abs, bias=col(THR + t))
+        tt(ref("Lh"), ref("Le"), full(5), A.mult)
+        tt(ref("Lx"), ref("Le"), full(4), A.mult)
+        wl = ref("b2", 0, 24)
+        wrap(wl, "WR", "Lh", True, True)
+        mm(full(1), B, ref("Lx"), True, True)
+        ts(ref("le"), wl, 2048.0, A.add)
+        ts(ref("hw"), wl, -16384.0, A.add)
+        act(ref("XB"), full(1), AF.Identity, bias=192.0 - 15.0 / 32.0, scale=1.0 / 16.0)
+        act(ref("XC"), ref("XB"), AF.Copy, scale=64.0)
+        mm(full(5), ref("FAm"), ref("Fm"), True, False)
+        mm(full(5), ref("FBm"), ref("Fm"), False, False)
+        mm(full(6), B, ref("Lx"), True, False)
+        mm(full(6), ref("NI16"), ref("XB"), False, True)
+
+        tt(ref("d"), ind(mngw, ref("le")), ref(m), A.subtract)
+        act(ref("ad"), ref("d"), AF.Abs)
+        tt(ref("LC"), ind(lexw, ref("le")), ref("Le"), A.mult)
+        act(ref("NP"), ref("nb"), AF.Relu, bias=64.0, scale=-2.0 ** 20)
+        act(ref("la"), full(6), AF.Abs, bias=col(PLM))
+        wl2 = ref("b7", 0, 24)
+        wrap(wl2, "WI", "XC", True, False)
+        for c in range(3):
+            o, fc = ref("b2", 8 * c, 8 * c + 8), ref("Fm", 128 * c, 128 * c + 128)
+            mm(o, fc, ref("WFA"), True, False)
+            mm(o, fc, ref("WFB"), False, False)
+            mm(o, ref("ad", 128 * c, 128 * c + 128), ref("B8"), False, True)
+        for c in range(3):
+            o, lxc, lcc = ref("b3", 8 * c, 8 * c + 8), ref("Lx", 128 * c, 128 * c + 128), ref("LC", 128 * c, 128 * c + 128)
+            mm(o, lxc, ref("MH"), True, False)
+            mm(o, lcc, ref("MH"), False, True)
+            o = ref("b3", 24 + 8 * c, 32 + 8 * c)
+            mm(o, lxc, ref("PH"), True, False)
+            mm(o, lcc, ref("MH"), False, True)
+        act(ref("mc"), ref("b3", 0, 24), AF.Copy)
+        act(ref("rc"), ref("b3", 24, 48), AF.Abs)
+        ts(ref("nf"), ref("b2", 0, 24), 4095.5, A.is_ge)
+        wrap(wl2, "WR", "LC", False, True)
+        mm(full(6), Id, ref("Lx"), True, False)
+        mm(full(6), Id, ref("NP"), False, True)
+        for q in range(24):
+            act(ref("ab", 64 * q, 64 * q + 64), ref("i64"), AF.Abs, bias=ref("mc", q, q + 1))
+        act(ref("lh"), ref("la"), AF.Relu, bias=1.0, scale=-1.0)
+        if t == 0:
+            picks("WG", "ge")
+        mm(full(5), B, ref("ad"), False, False)
+
+        for q in range(24):
+            u = ref("U", 64 * q, 64 * q + 64)
+            ts(u, ref("ab", 64 * q, 64 * q + 64), ref("rc", q, q + 1), A.is_equal, ref("nf", q, q + 1), A.mult)
+            mm(ref("b1", 0, 64, p=64), u, u, q == 0, q == 23)
+            if q == 11:
+                ts(ref("lf"), wl2, -12288.0, A.add)
+        tt(ref("LCm"), ref("LC"), full(6), A.min)
+        ts(ref("TS", p=64), ref("b1", 0, 64, p=64), 1.0, A.min)
+        for b in range(4):
+            mm(ref("b2", 64 * b, 64 * b + 64), ref("SEL", 128 * b, 128 * b + 128, p=64), ref("TS", p=64), True, True)
+        mm(full(0), Id, ref(x), True, False)
+        mm(full(0), ref("MI"), ref("NP"), False, True)
+        mm(full(4), Id, ref(x), True, False)
+        mm(full(4), ref("MI"), ref("Lx"), False, False)
+        ts(ref("hd"), ref("d"), 0.5, A.mult, -0.25, A.add)
+        cp(ref("TW"), ref("b2", 0, 256))
+        tt(ref("RF"), ind(ref("TW"), ref("lf")), ref("lh"), A.mult)
+        mm(full(5), ref("FLM"), ref("RF"), False, True)
+        mm(full(4), Id, ref("LCm"), False, True)
+        mm(full(3), B, ref("Lh"), True, True)
+        wl3 = ref("b2", 0, 24)
+        mm(full(6), Id, ref(m), True, False)
+
+        act(ref("nM"), full(5), AF.Relu, bias=64.0, scale=64.0)
+        act(ref("M"), ref("nM"), AF.Relu, bias=16384.0, scale=-256.0)
+        act(full(1), ref("M"), AF.Copy)
+        tt(ref("tx"), ref("nM"), full(0), A.min)
+        tt(ref(xn), ref("tx"), full(4), A.max)
+        send(ref(xn), ref("x%d" % (t + 1)), to, "ax%d" % (t + 1))
+        cp(ref("Hb"), full(3))
+        wrap(wl3, "WI", "M", True, True)
+        tt(ref("gd"), ref("hd"), full(1), A.mult)
+        tt(ref("hp"), ref("hw"), wl3, A.add)
+        mm(full(6), ref("I14"), ref("gd"), False, True)
+        act(ref(gn), full(6), AF.Copy)
+        send(ref(gn), ref("m%d" % (t + 1)), to, "ag%d" % (t + 1))
+        for q in range(24):
+            n, e = K - 16 * q, 384 * q
+            ts(ref("E", e, e + n), ref("Hb", 16 * q, K), ref("hp", q, q + 1), A.is_equal)
+            mm(ref("b7", 16 * q, K), B, ref("E", e, e + n), q == 0, q == 23)
+        act(ref("LB"), full(7), AF.Copy, scale=-65536.0)
+        wl4 = ref("b6", 0, 24)
+        for r in range(16):
+            mm(wl4, ref("WG", 128 * r, 128 * r + 128), ref("E", r, 24 * K, K), r == 0, False)
+        wrap(wl4, "WI", "LB", False, True)
+        if not last:
+            hash_s(t + 1, 0)
+            spread(t + 1, 0, False)
+        tt(ref("z"), ref("hp"), wl4, A.add)
+        ts(ref("z1"), ref("z"), -2048.5, A.is_ge, -16384.0, A.mult)
+        tt(ref("z2"), ref("z1"), ref("cim"), A.add)
+        tt(ref("z3"), ref("z"), ref("z2"), A.max)
+        ts(ref("lo"), ref("z3"), 2048.0, A.add)
+        scatter("lx", xn)
+        if last:
+            store("y", T.yl[:, :], lexw, "ol")
+            scatter("mn", gn)
+        else:
+            hash_v(0)
+
+    half = W // 2
+    act(ref("D", 0, half), ref("mn", 0, half), AF.Copy, accum=ref("ya"))
+    do("v", lambda: g.vector.tensor_reduce(ref("yb")[3], ref("mn", half, W)[3], AxisListType.X, A.add), [ref("mn", half, W)], [ref("yb")])
+    tt(ref("ys"), ref("ya"), ref("yb"), A.add)
+    store("y", T.yx[:, :], ref("x3"), "ox")
+    store("y", T.yg[:, :], ref("m3"), "og")
+    store("y", T.ym[:, :], ref("ys"), "om")
+    for q in ("v", "s", "t", "g"):
+        g.wait_ge(T.sem[own[q]], cnt[q])
+    g.wait_ge(T.sem["rl"], sent[0])
+    for s in ("ox", "og", "ol", "om"):
+        g.wait_ge(T.sem[s], 16)

@@ -50,7 +50,10 @@ def rank_program(g, core, T, topo):
 
     def ref(name, lo=0, hi=None, step=1, p=128):
         hi = T[name].shape[1] if hi is None else hi
-        return (name, lo, hi, T[name][0:p, lo:hi:step] if step != 1 else T[name][0:p, lo:hi])
+        return (name, lo, hi, T[name][0:p, lo:hi:step] if step != 1 else T[name][0:p, lo:hi], step)
+
+    def meet(lo, hi, st, l2, h2, s2):
+        return lo < h2 and l2 < hi and not (st == s2 and st > 1 and (lo - l2) % st)
 
     def is_ps(name):
         return name in SCRATCH and SCRATCH[name][0] == "psum"
@@ -59,12 +62,12 @@ def rank_program(g, core, T, topo):
         me = own.get(q)
         dep = {}
         for rs, w in ((reads, False), (writes, True)):
-            for (name, lo, hi, _) in rs:
-                for (l2, h2, ev, c, w2) in acc.get(name, []):
+            for (name, lo, hi, _, st) in rs:
+                for (l2, h2, ev, c, w2, s2) in acc.get(name, []):
                     if is_ps(name):
                         hit = ev != me or (q != "t" and (w or w2) and l2 < hi and lo < h2)
                     else:
-                        hit = l2 < hi and lo < h2 and (w or w2)
+                        hit = (w or w2) and meet(lo, hi, st, l2, h2, s2)
                     if hit and dep.get(ev, 0) < c:
                         dep[ev] = c
         todo = {e: c for e, c in dep.items() if known[q].get(e, 0) < c}
@@ -83,13 +86,16 @@ def rank_program(g, core, T, topo):
         k[ev] = c
         past[(ev, c)] = k
         for rs, w in ((reads, False), (writes, True)):
-            for (name, lo, hi, _) in rs:
+            for (name, lo, hi, _, st) in rs:
                 old = acc.get(name, [])
+
+                def inside(o):
+                    return lo <= o[0] and o[1] <= hi and (st == 1 or (st == o[5] and (lo - o[0]) % st == 0))
                 if w:
-                    old = [o for o in old if not (lo <= o[0] and o[1] <= hi) or (is_ps(name) and o[2] != ev)]
+                    old = [o for o in old if not inside(o) or (is_ps(name) and o[2] != ev)]
                 else:
-                    old = [o for o in old if not (o[2] == ev and not o[4] and lo <= o[0] and o[1] <= hi)]
-                acc[name] = old + [(lo, hi, ev, c, w)]
+                    old = [o for o in old if not (o[2] == ev and not o[4] and inside(o))]
+                acc[name] = old + [(lo, hi, ev, c, w, st)]
 
     def do(q, fn, reads, writes):
         need(q, reads, writes)
@@ -106,10 +112,10 @@ def rank_program(g, core, T, topo):
         return out
 
     def ap(x):
-        return x[-1] if isinstance(x, tuple) else x
+        return x[3] if isinstance(x, tuple) else x
 
     def ind(win, off):
-        return (None, [win, off], win[3].indirect(off[3]))
+        return (None, [win, off], None, win[3].indirect(off[3]))
 
     def tt(out, a, b, op):
         do("v", lambda: g.vector.tensor_tensor(ap(out), ap(a), ap(b), op), rd(a, b), rd(out))
@@ -177,7 +183,7 @@ def rank_program(g, core, T, topo):
     iota(ref("cg"), [[1, 8], [0, 16]], 0, 0)
     iota(ref("cl"), [[0, 8], [1, 16]], 0, 0)
     iota(ref("i64"), [[1, 64]], 0, 0)
-    iota(ref("ci"), [[16, 24]], 2048, 0)
+    iota(ref("ci"), [[16, 24]], 4096, 0)
     iota(ref("wr3"), [[-100, 16], [1, 8], [100, 16]], 0, 0)
     iota(ref("sbi"), [[16, 4], [0, 8], [1, 16]], 0, 0)
 
@@ -241,7 +247,7 @@ def rank_program(g, core, T, topo):
         ts(ref("SEL", p=64), ref("sbi", p=64), ref("col", PP, PP + 1, p=64), A.is_equal)
         ts(ref("cim"), ref("ci"), col(PL), A.add)
         ts(col(PLM), col(PL), -1.0, A.mult, 3072.0, A.add)
-        ts(ref("ge"), ref("cl", 0, 16), col(PL), A.is_le, 65536.0, A.mult)
+        ts(ref("ge"), ref("cl", 0, 16), col(PL), A.is_le, -65536.0, A.mult)
 
     def full(b, n=K):
         return ref("b%d" % b, 0, n)
@@ -289,11 +295,17 @@ def rank_program(g, core, T, topo):
     def hash_v(b):
         i0, i1 = HBL[b]
         n = i1 - i0
-        tt(ref("pr", 0, n), ref("UP", 0, n), full(1, n), A.mult)
-        ts(ref("ps", 0, n), ref("pr", 0, n), 5, A.arith_shift_right)
-        tt(ref("pt", 0, n), ref("ps", 0, n), full(1, n), A.add)
-        ts(ref("hi", i0, i1), ref("pt", 0, n), 4095, A.bitwise_and)
-        cp(ref("hu", i0, i1), ref("hi", i0, i1))
+        hv = [(0, n // 2), (n // 2, n)]
+        for a, e in hv:
+            tt(ref("pr", a, e), ref("UP", a, e), ref("b1", a, e), A.mult)
+        for a, e in hv:
+            ts(ref("ps", a, e), ref("pr", a, e), 5, A.arith_shift_right)
+        for a, e in hv:
+            tt(ref("pt", a, e), ref("ps", a, e), ref("b1", a, e), A.add)
+        for a, e in hv:
+            ts(ref("hi", i0 + a, i0 + e), ref("pt", a, e), 4095, A.bitwise_and)
+        for a, e in hv:
+            cp(ref("hu", i0 + a, i0 + e), ref("hi", i0 + a, i0 + e))
 
     def look(b):
         i0, i1 = BLK[b]
@@ -440,6 +452,7 @@ def rank_program(g, core, T, topo):
         wrap(wl3, "WI", "M", True, True)
         tt(ref("gd"), ref("hd"), full(1), A.mult)
         tt(ref("hp"), ref("hw"), wl3, A.add)
+        ts(ref("z3"), wl3, -2.0, A.mult, 34816.0, A.add)
         mm(full(6), ref("I14"), ref("gd"), False, True)
         act(ref(gn), full(6), AF.Copy)
         send(ref(gn), ref("m%d" % (t + 1)), to, "ag%d" % (t + 1))
@@ -447,7 +460,11 @@ def rank_program(g, core, T, topo):
             n, e = K - 16 * q, 384 * q
             ts(ref("E", e, e + n), ref("Hb", 16 * q, K), ref("hp", q, q + 1), A.is_equal)
             mm(ref("b7", 16 * q, K), B, ref("E", e, e + n), q == 0, q == 23)
-        act(ref("LB"), full(7), AF.Copy, scale=-65536.0)
+            if q == 5:
+                tt(ref("z3"), ref("z3"), ref("hp"), A.add)
+            if q == 11:
+                tt(ref("z"), ref("z3"), ref("cim"), A.min)
+        act(ref("LB"), full(7), AF.Copy, scale=65536.0)
         wl4 = ref("b6", 0, 24)
         for r in range(16):
             mm(wl4, ref("WG", 128 * r, 128 * r + 128), ref("E", r, 24 * K, K), r == 0, False)
@@ -455,11 +472,9 @@ def rank_program(g, core, T, topo):
         if not last:
             hash_s(t + 1, 0)
             spread(t + 1, 0, False)
-        tt(ref("z"), ref("hp"), wl4, A.add)
-        ts(ref("z1"), ref("z"), -2048.5, A.is_ge, -16384.0, A.mult)
-        tt(ref("z2"), ref("z1"), ref("cim"), A.add)
-        tt(ref("z3"), ref("z"), ref("z2"), A.max)
-        ts(ref("lo"), ref("z3"), 2048.0, A.add)
+        tt(ref("z1"), ref("cim"), wl4, A.min)
+        tt(ref("z2"), ref("z1"), ref("z"), A.max)
+        cp(ref("lo"), ref("z2"))
         scatter("lx", xn)
         if last:
             store("y", T.yl[:, :], lexw, "ol")

@@ -1,23 +1,23 @@
 from concourse.mybir import dt, AluOpType, AxisListType, ActivationFunctionType
 
 N, W, K, VIS = 6, 4096, 384, 3
-HBL = [(0, 128), (128, 384)]
-BLK = [(0, 128), (128, 256), (256, 320), (320, 384)]
+HBL = [(0, 192), (192, 384)]
+BLK = [(0, 128), (192, 320), (320, 384), (128, 192)]
 NENG = 8
 BF, F32, I32, U16, F16 = "bfloat16", "float32", "int32", "uint16", "float16"
 SCRATCH = {
     "lx": ("sbuf", [128, W + K], BF), "mn": ("sbuf", [128, W + K], BF),
     "wti": ("sbuf", [128, 2], I32), "thi": ("sbuf", [128, 1], I32), "pi": ("sbuf", [128, 1], I32), "pj": ("sbuf", [128, 4], I32),
-    "col": ("sbuf", [128, 24], F32), "i64": ("sbuf", [128, 64], BF), "one": ("sbuf", [128, 256], BF), "neg": ("sbuf", [128, 64], BF), "C": ("sbuf", [128, 1024], BF), "CA": ("sbuf", [128, 1024], BF), "la": ("sbuf", [128, K], BF),
+    "col": ("sbuf", [128, 24], F32), "i64": ("sbuf", [128, 64], BF), "zz": ("sbuf", [128, 48], BF), "one": ("sbuf", [128, 256], BF), "neg": ("sbuf", [128, 64], BF), "C": ("sbuf", [128, 1024], BF), "CA": ("sbuf", [128, 1024], BF), "la": ("sbuf", [128, K], BF),
     "X16": ("sbuf", [128, 16 * K], BF), "D": ("sbuf", [128, 16 * K], BF), "E": ("sbuf", [128, 24 * K], BF), "UP": ("sbuf", [128, 256], F32), "Mh": ("sbuf", [128, 512], BF),
     "hi": ("sbuf", [128, K], I32), "hu": ("sbuf", [128, K], U16), "hd": ("sbuf", [128, K], I32), "Lh": ("sbuf", [128, K], F16), "Hb": ("sbuf", [128, K], F16),
     "le": ("sbuf", [128, 24], U16), "lf": ("sbuf", [128, 24], U16), "lo": ("sbuf", [128, 24], U16),
     "ab": ("sbuf", [128, 1536], BF), "U": ("sbuf", [128, 1536], BF), "TS": ("sbuf", [128, 64], BF), "TW": ("sbuf", [128, 256], BF),
-    "ya": ("sbuf", [128, 1], F32), "yb": ("sbuf", [128, 1], F32), "ys": ("sbuf", [128, 1], F32),
+    "ya": ("sbuf", [128, 1], F32), "yb": ("sbuf", [128, 1], F32),
 }
-for _n in ("x0 x1 x2 x3 m0 m1 m2 m3 xn0 xn1 xn2 gn0 gn1 gn2 pm Le Fm nb NP Lx d ad LC LCm XB XC lh RF tx M nM gd LB").split():
+for _n in ("x0 x1 x2 x3 m0 m1 m2 m3 xn0 xn1 xn2 gn0 gn1 gn2 pm Le Fm nb NP Lx d ad LC LCm XB XC lh RF tx M XT gd LB").split():
     SCRATCH[_n] = ("sbuf", [128, K], BF)
-for _n in ("cg cl cq B Id BmI up L Lm Gm Wv0 Wv1 Wv2 Wa Wb C6 NI4 MI NI16 I14 FLM FAm FBm").split():
+for _n in ("cg cl cq B Id BmI up L Lm Gm Wv0 Wv1 Wv2 Wa Wb C6 NI4 MI NI16 I14 FLM B64 FAm FBm").split():
     SCRATCH[_n] = ("sbuf", [128, 128], BF)
 for _n in ("B8 PH MH WFA WFB").split():
     SCRATCH[_n] = ("sbuf", [128, 8], BF)
@@ -195,6 +195,7 @@ def rank_program(g, core, T, topo):
     ts(ref("pj", 1, 2), ref("pi"), 15, A.bitwise_and)
     fill(ref("C6"), 6144.0)
     fill(ref("one"), 1.0)
+    fill(ref("zz"), 0.0)
     fill(ref("neg"), -1.0 / 128)
     cp(col(PG), ref("pj", 0, 1))
     cp(col(PL), ref("pj", 1, 2))
@@ -215,7 +216,7 @@ def rank_program(g, core, T, topo):
 
     def more_constants():
         for name, src, s in (("MI", "Id", -1.0), ("NI16", "Id", -16.0),
-                             ("I14", "Id", 2.0 ** -14), ("FLM", "B", 4096.0), ("PH", "B8", 0.5), ("MH", "B8", -0.5)):
+                             ("I14", "Id", 2.0 ** -14), ("FLM", "B", 2.0 ** 18), ("B64", "B", 64.0), ("PH", "B8", 0.5), ("MH", "B8", -0.5)):
             act(ref(name), ref(src), AF.Copy, scale=s)
         act(ref("CN"), ref("CK"), AF.Copy, scale=-1.0)
 
@@ -226,27 +227,35 @@ def rank_program(g, core, T, topo):
 
     def v_constants():
         ts(ref("up"), ref("cl"), col(PL), A.is_gt)
-        tt(ref("L"), ref("up"), B, A.mult)
-        ts(ref("Lm"), ref("L"), -128.0, A.mult)
-        tt(ref("Gm"), ref("BmI"), ref("L"), A.subtract)
-        ts(ref("Gm"), ref("Gm"), 2.0 ** -14, A.mult)
-        for t in range(VIS):
-            w = "Wv%d" % t
-            tt(ref(w), ref("Lm"), Id, A.add)
-            tt(ref(w, t, 128, 16), ref(w, t, 128, 16), ref("Gm", t, 128, 16), A.subtract)
-            ts(col(THR + t), col(PL), float(t), A.not_equal)
-        ts(ref("WR"), ref("wr3"), col(PG), A.is_equal)
         ts(ref("pj", 2, 3), ref("thi"), 4, A.arith_shift_right)
         ts(ref("pj", 3, 4), ref("thi"), 15, A.bitwise_and)
+        ts(col(THR), col(PL), 0.0, A.not_equal)
+        tt(ref("L"), ref("up"), B, A.mult)
+        ts(ref("WR"), ref("wr3"), col(PG), A.is_equal)
         cp(ref("col", THA, THA + 2), ref("pj", 2, 4))
+        ts(ref("Lm"), ref("L"), -128.0, A.mult)
+        tt(ref("Gm"), ref("BmI"), ref("L"), A.subtract)
+        ts(col(PLM), col(PL), -1.0, A.mult, 3072.0, A.add)
         ts(col(C_FAM), col(THA), -16.0, A.mult)
         ts(col(C_FBM), col(THB), -1.0, A.mult)
+        tt(ref("Wv0"), ref("Lm"), Id, A.add)
+        ts(ref("Gm"), ref("Gm"), 2.0 ** -14, A.mult)
         ts(col(C_WA), col(THA), -16.0, A.mult, 4096.0, A.add)
-        for name, src, c in (("FAm", "B", C_FAM), ("FBm", "B", C_FBM), ("WFA", "B8", C_WA), ("WFB", "B8", C_FBM)):
-            ts(ref(name), ref(src), col(c), A.mult)
+        ts(ref("FAm"), B, col(C_FAM), A.mult, 64.0, A.mult)
+        ts(ref("FBm"), B, col(C_FBM), A.mult, 64.0, A.mult)
+        tt(ref("Wv0", 0, 128, 16), ref("Wv0", 0, 128, 16), ref("Gm", 0, 128, 16), A.subtract)
+        ts(ref("WFA"), ref("B8"), col(C_WA), A.mult)
+        ts(ref("WFB"), ref("B8"), col(C_FBM), A.mult)
+
+    def late_constants():
+        for t in range(1, VIS):
+            tt(ref("Wv%d" % t), ref("Lm"), Id, A.add)
+            ts(col(THR + t), col(PL), float(t), A.not_equal)
         ts(ref("SEL", p=64), ref("sbi", p=64), ref("col", PP, PP + 1, p=64), A.is_equal)
+        for t in range(1, VIS):
+            w = ref("Wv%d" % t, t, 128, 16)
+            tt(w, w, ref("Gm", t, 128, 16), A.subtract)
         ts(ref("cim"), ref("ci"), col(PL), A.add)
-        ts(col(PLM), col(PL), -1.0, A.mult, 3072.0, A.add)
         ts(ref("ge"), ref("cl", 0, 16), col(PL), A.is_le, -65536.0, A.mult)
 
     def full(b, n=K):
@@ -307,10 +316,11 @@ def rank_program(g, core, T, topo):
         for a, e in hv:
             cp(ref("hu", i0 + a, i0 + e), ref("hi", i0 + a, i0 + e))
 
-    def look(b):
+    def pick(i0, i1):
+        tt(ref("D", 16 * i0, 16 * i1), ind(lexw, ref("hu", i0, i1)), ref("X16", 16 * i0, 16 * i1), A.not_equal)
+
+    def count(b):
         i0, i1 = BLK[b]
-        dd = ref("D", 16 * i0, 16 * i1)
-        tt(dd, ind(lexw, ref("hu", i0, i1)), ref("X16", 16 * i0, 16 * i1), A.not_equal)
         for k in range(16):
             mm(ref("b3", i0, i1), ref("CK", 128 * k, 128 * k + 128), ref("D", 16 * i0 + k, 16 * i1, 16), k == 0, k == 15)
 
@@ -324,6 +334,8 @@ def rank_program(g, core, T, topo):
                 c = ref("b%d" % (6 + h), n * k, n * k + n)
                 mm(c, ref("MI"), ref("x%d" % t, i0, i1), True, False)
                 mm(c, Id, ref("C", 8 * h + k, 1024, 16), False, True)
+
+    def unlike_s():
         for h in range(2):
             act(ref("CA", 512 * h, 512 * h + 512), full(6 + h, 512), AF.Abs)
         act(ref("C"), ref("CA"), AF.Relu, bias=1.0, scale=-1.0)
@@ -350,125 +362,151 @@ def rank_program(g, core, T, topo):
         to = (rank + 2) % N if last else (rank - 1) % N
 
         hash_s(t, 1)
-        look(0)
+        i0, i1 = HBL[1]
+        n = i1 - i0
+        pick(0, 32)
+        tt(ref("pr", 0, n), ref("UP", 0, n), full(1, n), A.mult)
+        pick(32, 64)
+        ts(ref("ps", 0, n), ref("pr", 0, n), 5, A.arith_shift_right)
+        pick(64, 96)
+        tt(ref("pt", 0, n), ref("ps", 0, n), full(1, n), A.add)
+        pick(96, 128)
+        ts(ref("hi", i0, i1), ref("pt", 0, n), 4095, A.bitwise_and)
+        ts(full(5, i0), ref("hi", 0, i0), -2048.0, A.add)
+        cp(ref("hu", i0, i1), ref("hi", i0, i1))
+        count(0)
         spread(t, 1, False)
         if t == 0:
             more_constants()
-        hash_v(1)
-        spread(t, 2, False)
         look_s(t, 3)
+        spread(t, 2, False)
+        unlike_s()
         act(full(4), ref(x), AF.Copy)
-        look(1)
+        pick(*BLK[1])
+        count(1)
         count_s(3)
-        look(2)
+        pick(*BLK[2])
+        count(2)
         if t == 0:
             v_constants()
             picks("WI", "eq")
-        ts(full(5), ref("hi"), -2048.0, A.add)
+        ts(ref("b5", i0, i1), ref("hi", i0, i1), -2048.0, A.add)
         if t > 0:
             scatter("mn", "gn%d" % (t - 1))
 
         ts(ref("pm"), full(3), -13.5, A.is_le)
         mm(full(0), ref("Wv%d" % t), ref("pm"), True, True)
-        ts(ref("Le"), full(0), col(THR + t), A.is_ge)
-        act(ref("Fm"), full(0), AF.Relu)
+        halves = [(0, K // 2), (K // 2, K)]
+        for a, e in halves:
+            ts(ref("Le", a, e), ref("b0", a, e), col(THR + t), A.is_ge)
         act(ref("nb"), full(0), AF.Abs, bias=col(THR + t))
-        tt(ref("Lh"), ref("Le"), full(5), A.mult)
+        act(ref("Fm"), full(0), AF.Relu)
+        for a, e in halves:
+            tt(ref("Lh", a, e), ref("Le", a, e), ref("b5", a, e), A.mult)
         tt(ref("Lx"), ref("Le"), full(4), A.mult)
         wl = ref("b2", 0, 24)
         wrap(wl, "WR", "Lh", True, True)
         mm(full(1), B, ref("Lx"), True, True)
+        act(ref("NP"), ref("nb"), AF.Relu, bias=64.0, scale=-2.0 ** 20)
         ts(ref("le"), wl, 2048.0, A.add)
         ts(ref("hw"), wl, -16384.0, A.add)
         act(ref("XB"), full(1), AF.Identity, bias=192.0 - 15.0 / 32.0, scale=1.0 / 16.0)
-        act(ref("XC"), ref("XB"), AF.Copy, scale=64.0)
-        mm(full(5), ref("FAm"), ref("Fm"), True, False)
-        mm(full(5), ref("FBm"), ref("Fm"), False, False)
-        mm(full(6), B, ref("Lx"), True, False)
-        mm(full(6), ref("NI16"), ref("XB"), False, True)
+        wm = ref("b2", 0, 24)
+        mm(wm, B, ref("zz", 0, 24), True, False)
+        for c in range(3):
+            o, fc = ref("b2", 8 * c, 8 * c + 8), ref("Fm", 128 * c, 128 * c + 128)
+            mm(o, fc, ref("WFA"), False, False)
+            mm(o, fc, ref("WFB"), False, False)
+        mm(ref("b3", 0, 48), B, ref("zz"), True, False)
+        for c in range(3):
+            lxc = ref("Lx", 128 * c, 128 * c + 128)
+            mm(ref("b3", 8 * c, 8 * c + 8), lxc, ref("MH"), False, False)
+            mm(ref("b3", 24 + 8 * c, 32 + 8 * c), lxc, ref("PH"), False, False)
+        mm(full(6), Id, ref("Lx"), True, False)
+        mm(full(6), Id, ref("NP"), False, True)
+        mm(full(0), Id, ref(x), True, False)
+        mm(full(0), ref("MI"), ref("NP"), False, True)
 
         tt(ref("d"), ind(mngw, ref("le")), ref(m), A.subtract)
         act(ref("ad"), ref("d"), AF.Abs)
         tt(ref("LC"), ind(lexw, ref("le")), ref("Le"), A.mult)
-        act(ref("NP"), ref("nb"), AF.Relu, bias=64.0, scale=-2.0 ** 20)
-        act(ref("la"), full(6), AF.Abs, bias=col(PLM))
+        act(ref("XC"), ref("XB"), AF.Copy, scale=64.0)
+        if t == 0:
+            late_constants()
         wl2 = ref("b7", 0, 24)
-        wrap(wl2, "WI", "XC", True, False)
         for c in range(3):
-            o, fc = ref("b2", 8 * c, 8 * c + 8), ref("Fm", 128 * c, 128 * c + 128)
-            mm(o, fc, ref("WFA"), True, False)
-            mm(o, fc, ref("WFB"), False, False)
-            mm(o, ref("ad", 128 * c, 128 * c + 128), ref("B8"), False, True)
+            mm(ref("b2", 8 * c, 8 * c + 8), ref("ad", 128 * c, 128 * c + 128), ref("B8"), False, c == 2)
         for c in range(3):
-            o, lxc, lcc = ref("b3", 8 * c, 8 * c + 8), ref("Lx", 128 * c, 128 * c + 128), ref("LC", 128 * c, 128 * c + 128)
-            mm(o, lxc, ref("MH"), True, False)
-            mm(o, lcc, ref("MH"), False, True)
-            o = ref("b3", 24 + 8 * c, 32 + 8 * c)
-            mm(o, lxc, ref("PH"), True, False)
-            mm(o, lcc, ref("MH"), False, True)
+            lcc = ref("LC", 128 * c, 128 * c + 128)
+            mm(ref("b3", 8 * c, 8 * c + 8), lcc, ref("MH"), False, False)
+            mm(ref("b3", 24 + 8 * c, 32 + 8 * c), lcc, ref("MH"), False, c == 2)
         act(ref("mc"), ref("b3", 0, 24), AF.Copy)
         act(ref("rc"), ref("b3", 24, 48), AF.Abs)
+        ts(ref("hd"), ref("d"), 0.5, A.mult, -0.25, A.add)
+        tt(ref("LCm"), ref("LC"), full(6), A.min)
         ts(ref("nf"), ref("b2", 0, 24), 4095.5, A.is_ge)
-        wrap(wl2, "WR", "LC", False, True)
-        mm(full(6), Id, ref("Lx"), True, False)
-        mm(full(6), Id, ref("NP"), False, True)
+        wrap(wl2, "WI", "XC", True, False)
         for q in range(24):
             act(ref("ab", 64 * q, 64 * q + 64), ref("i64"), AF.Abs, bias=ref("mc", q, q + 1))
-        act(ref("lh"), ref("la"), AF.Relu, bias=1.0, scale=-1.0)
-        if t == 0:
-            picks("WG", "ge")
-        mm(full(5), B, ref("ad"), False, False)
 
         for q in range(24):
             u = ref("U", 64 * q, 64 * q + 64)
             ts(u, ref("ab", 64 * q, 64 * q + 64), ref("rc", q, q + 1), A.is_equal, ref("nf", q, q + 1), A.mult)
             mm(ref("b1", 0, 64, p=64), u, u, q == 0, q == 23)
-            if q == 11:
-                ts(ref("lf"), wl2, -12288.0, A.add)
-        tt(ref("LCm"), ref("LC"), full(6), A.min)
+            if q == 7:
+                mm(full(6), B, ref("Lx"), True, False)
+                mm(full(6), ref("NI16"), ref("XB"), False, True)
+        act(ref("XT"), full(0), AF.Copy)
+        act(ref("la"), full(6), AF.Abs, bias=col(PLM))
+        wrap(wl2, "WR", "LC", False, True)
         ts(ref("TS", p=64), ref("b1", 0, 64, p=64), 1.0, A.min)
+        ts(ref("lf"), wl2, -12288.0, A.add)
         for b in range(4):
             mm(ref("b2", 64 * b, 64 * b + 64), ref("SEL", 128 * b, 128 * b + 128, p=64), ref("TS", p=64), True, True)
-        mm(full(0), Id, ref(x), True, False)
-        mm(full(0), ref("MI"), ref("NP"), False, True)
-        mm(full(4), Id, ref(x), True, False)
-        mm(full(4), ref("MI"), ref("Lx"), False, False)
-        ts(ref("hd"), ref("d"), 0.5, A.mult, -0.25, A.add)
+        act(ref("lh"), ref("la"), AF.Relu, bias=1.0, scale=-1.0)
+        if t == 0:
+            picks("WG", "ge")
+        mm(full(3), B, ref("Lh"), True, True)
+        for lw, src in (("B64", "Le"), ("FAm", "Fm"), ("FBm", "Fm"), ("B64", "ad")):
+            mm(full(5), ref(lw), ref(src), src == "Le", False)
         cp(ref("TW"), ref("b2", 0, 256))
         tt(ref("RF"), ind(ref("TW"), ref("lf")), ref("lh"), A.mult)
+        cp(ref("Hb"), full(3))
         mm(full(5), ref("FLM"), ref("RF"), False, True)
+        mm(full(4), Id, ref(x), True, False)
+        mm(full(4), ref("MI"), ref("Lx"), False, False)
         mm(full(4), Id, ref("LCm"), False, True)
-        mm(full(3), B, ref("Lh"), True, True)
         wl3 = ref("b2", 0, 24)
         mm(full(6), Id, ref(m), True, False)
 
-        act(ref("nM"), full(5), AF.Relu, bias=64.0, scale=64.0)
-        act(ref("M"), ref("nM"), AF.Relu, bias=16384.0, scale=-256.0)
-        act(full(1), ref("M"), AF.Copy)
-        tt(ref("tx"), ref("nM"), full(0), A.min)
-        tt(ref(xn), ref("tx"), full(4), A.max)
-        send(ref(xn), ref("x%d" % (t + 1)), to, "ax%d" % (t + 1))
-        cp(ref("Hb"), full(3))
+        ts(ref("M"), full(5), 32.0, A.is_lt, 16384.0, A.mult)
         wrap(wl3, "WI", "M", True, True)
-        tt(ref("gd"), ref("hd"), full(1), A.mult)
+        act(full(1), ref("M"), AF.Copy)
+        for a, e in halves:
+            tt(ref("tx", a, e), ref("XT", a, e), ref("b5", a, e), A.min)
+        for a, e in halves:
+            tt(ref(xn, a, e), ref("tx", a, e), ref("b4", a, e), A.max)
+        send(ref(xn), ref("x%d" % (t + 1)), to, "ax%d" % (t + 1))
         tt(ref("hp"), ref("hw"), wl3, A.add)
         ts(ref("z3"), wl3, -2.0, A.mult, 34816.0, A.add)
-        mm(full(6), ref("I14"), ref("gd"), False, True)
-        act(ref(gn), full(6), AF.Copy)
-        send(ref(gn), ref("m%d" % (t + 1)), to, "ag%d" % (t + 1))
         for q in range(24):
             n, e = K - 16 * q, 384 * q
             ts(ref("E", e, e + n), ref("Hb", 16 * q, K), ref("hp", q, q + 1), A.is_equal)
             mm(ref("b7", 16 * q, K), B, ref("E", e, e + n), q == 0, q == 23)
             if q == 5:
                 tt(ref("z3"), ref("z3"), ref("hp"), A.add)
+            if q == 8:
+                tt(ref("gd"), ref("hd"), full(1), A.mult)
             if q == 11:
                 tt(ref("z"), ref("z3"), ref("cim"), A.min)
         act(ref("LB"), full(7), AF.Copy, scale=65536.0)
-        wl4 = ref("b6", 0, 24)
+        wl4 = ref("b5", 0, 24)
         for r in range(16):
             mm(wl4, ref("WG", 128 * r, 128 * r + 128), ref("E", r, 24 * K, K), r == 0, False)
         wrap(wl4, "WI", "LB", False, True)
+        mm(full(6), ref("I14"), ref("gd"), False, True)
+        act(ref(gn), full(6), AF.Copy)
+        send(ref(gn), ref("m%d" % (t + 1)), to, "ag%d" % (t + 1))
         if not last:
             hash_s(t + 1, 0)
             spread(t + 1, 0, False)
@@ -485,10 +523,10 @@ def rank_program(g, core, T, topo):
     half = W // 2
     act(ref("D", 0, half), ref("mn", 0, half), AF.Copy, accum=ref("ya"))
     do("v", lambda: g.vector.tensor_reduce(ref("yb")[3], ref("mn", half, W)[3], AxisListType.X, A.add), [ref("mn", half, W)], [ref("yb")])
-    tt(ref("ys"), ref("ya"), ref("yb"), A.add)
+    tt(ref("ya"), ref("ya"), ref("yb"), A.add)
     store("y", T.yx[:, :], ref("x3"), "ox")
     store("y", T.yg[:, :], ref("m3"), "og")
-    store("y", T.ym[:, :], ref("ys"), "om")
+    store("y", T.ym[:, :], ref("ya"), "om")
     for q in ("v", "s", "t", "g"):
         g.wait_ge(T.sem[own[q]], cnt[q])
     g.wait_ge(T.sem["rl"], sent[0])

from concourse.mybir import dt, AluOpType, AxisListType, ActivationFunctionType

N, W, K, VIS = 6, 4096, 384, 3
HBL = [(0, 192), (192, 384)]
BLK = [(0, 128), (192, 320), (320, 384), (128, 192)]
NENG = 8
BF, F32, I32, U16, F16 = "bfloat16", "float32", "int32", "uint16", "float16"
SCRATCH = {
    "lx": ("sbuf", [128, W + K], BF), "mn": ("sbuf", [128, W + K], BF),
    "wti": ("sbuf", [128, 2], I32), "thi": ("sbuf", [128, 1], I32), "pi": ("sbuf", [128, 1], I32), "pj": ("sbuf", [128, 4], I32),
    "col": ("sbuf", [128, 24], F32), "i64": ("sbuf", [128, 64], BF), "zz": ("sbuf", [128, 48], BF), "one": ("sbuf", [128, 256], BF), "neg": ("sbuf", [128, 64], BF), "C": ("sbuf", [128, 1024], BF), "CA": ("sbuf", [128, 1024], BF), "la": ("sbuf", [128, K], BF),
    "X16": ("sbuf", [128, 16 * K], BF), "D": ("sbuf", [128, 16 * K], BF), "E": ("sbuf", [128, 24 * K], BF), "UP": ("sbuf", [128, 256], F32), "Mh": ("sbuf", [128, 512], BF),
    "hi": ("sbuf", [128, K], I32), "hu": ("sbuf", [128, K], U16), "hd": ("sbuf", [128, K], I32), "Lh": ("sbuf", [128, K], F16), "Hb": ("sbuf", [128, K], F16),
    "le": ("sbuf", [128, 24], U16), "lf": ("sbuf", [128, 24], U16), "lo": ("sbuf", [128, 24], U16),
    "ab": ("sbuf", [128, 1536], BF), "U": ("sbuf", [128, 1536], BF), "TS": ("sbuf", [128, 64], BF), "TW": ("sbuf", [128, 256], BF),
    "ya": ("sbuf", [128, 1], F32), "yb": ("sbuf", [128, 1], F32),
}
for _n in ("x0 x1 x2 x3 m0 m1 m2 m3 xn0 xn1 xn2 gn0 gn1 gn2 pm Le Fm nb NP Lx d ad LC LCm XB XC lh RF tx M XT gd LB").split():
    SCRATCH[_n] = ("sbuf", [128, K], BF)
for _n in ("cg cl cq B Id BmI up L Lm Gm Wv0 Wv1 Wv2 Wa Wb C6 NI4 MI NI16 I14 FLM B64 FAm FBm").split():
    SCRATCH[_n] = ("sbuf", [128, 128], BF)
for _n in ("B8 PH MH WFA WFB").split():
    SCRATCH[_n] = ("sbuf", [128, 8], BF)
for _n in ("wr3 WR WI WG CK CN").split():
    SCRATCH[_n] = ("sbuf", [128, 2048], BF)
for _n in ("sbi SEL").split():
    SCRATCH[_n] = ("sbuf", [128, 512], BF)
for _n in ("pr ps pt").split():
    SCRATCH[_n] = ("sbuf", [128, 256], I32)
for _n in ("eq cw ge").split():
    SCRATCH[_n] = ("sbuf", [128, 16], F32)
for _n in ("ci cim mc rc nf hw hp z z1 z2 z3").split():
    SCRATCH[_n] = ("sbuf", [128, 24], F32)
for _b in range(8):
    SCRATCH["b%d" % _b] = ("psum", [128, 512], F32)
SEMAPHORES = ["qv", "qs", "qt", "qg", "lx", "lw", "lt", "lg", "ll", "lm", "ax1", "ag1", "ax2", "ag2", "ax3", "ag3", "rl", "ox", "og", "ol", "om"]


def rank_program(g, core, T, topo):
    rank = T.rank_of(core)
    if rank is None:
        return
    A, AF = AluOpType, ActivationFunctionType
    Q = {"v": g.vector, "s": g.scalar, "t": g.tensor, "g": g, "y": g.sync}
    own = {"v": "qv", "s": "qs", "t": "qt", "g": "qg"}
    cnt = {"v": 0, "s": 0, "t": 0, "g": 0}
    known = {q: {} for q in Q}
    past = {}
    acc = {}

    def ref(name, lo=0, hi=None, step=1, p=128):
        hi = T[name].shape[1] if hi is None else hi
        return (name, lo, hi, T[name][0:p, lo:hi:step] if step != 1 else T[name][0:p, lo:hi], step)

    def meet(lo, hi, st, l2, h2, s2):
        return lo < h2 and l2 < hi and not (st == s2 and st > 1 and (lo - l2) % st)

    def is_ps(name):
        return name in SCRATCH and SCRATCH[name][0] == "psum"

    def need(q, reads, writes):
        me = own.get(q)
        dep = {}
        for rs, w in ((reads, False), (writes, True)):
            for (name, lo, hi, _, st) in rs:
                for (l2, h2, ev, c, w2, s2) in acc.get(name, []):
                    if is_ps(name):
                        hit = ev != me or (q != "t" and (w or w2) and l2 < hi and lo < h2)
                    else:
                        hit = (w or w2) and meet(lo, hi, st, l2, h2, s2)
                    if hit and dep.get(ev, 0) < c:
                        dep[ev] = c
        todo = {e: c for e, c in dep.items() if known[q].get(e, 0) < c}
        for e in list(todo):
            if any(f != e and past.get((f, todo[f]), {}).get(e, 0) >= todo[e] for f in todo):
                del todo[e]
        for e, c in todo.items():
            Q[q].wait_ge(T.sem[e], c)
            k = known[q]
            k[e] = max(k.get(e, 0), c)
            for e2, c2 in past.get((e, c), {}).items():
                k[e2] = max(k.get(e2, 0), c2)

    def note(ev, c, q, reads, writes):
        k = dict(known[q]) if q else {}
        k[ev] = c
        past[(ev, c)] = k
        for rs, w in ((reads, False), (writes, True)):
            for (name, lo, hi, _, st) in rs:
                old = acc.get(name, [])

                def inside(o):
                    return lo <= o[0] and o[1] <= hi and (st == 1 or (st == o[5] and (lo - o[0]) % st == 0))
                if w:
                    old = [o for o in old if not inside(o) or (is_ps(name) and o[2] != ev)]
                else:
                    old = [o for o in old if not (o[2] == ev and not o[4] and inside(o))]
                acc[name] = old + [(lo, hi, ev, c, w, st)]

    def do(q, fn, reads, writes):
        need(q, reads, writes)
        ins = fn()
        cnt[q] += 1
        ins.then_inc(T.sem[own[q]], 1)
        note(own[q], cnt[q], q, reads, writes)

    def rd(*xs):
        out = []
        for x in xs:
            if isinstance(x, tuple):
                out += x[1] if x[0] is None else [x]
        return out

    def ap(x):
        return x[3] if isinstance(x, tuple) else x

    def ind(win, off):
        return (None, [win, off], None, win[3].indirect(off[3]))

    def tt(out, a, b, op):
        do("v", lambda: g.vector.tensor_tensor(ap(out), ap(a), ap(b), op), rd(a, b), rd(out))

    def ts(out, a, s1, op0, s2=None, op1=None):
        if op1 is None:
            do("v", lambda: g.vector.tensor_scalar(ap(out), ap(a), ap(s1), None, op0), rd(a, s1), rd(out))
        else:
            do("v", lambda: g.vector.tensor_scalar(ap(out), ap(a), ap(s1), ap(s2), op0, op1), rd(a, s1, s2), rd(out))

    def cp(out, a):
        do("v", lambda: g.vector.tensor_copy(ap(out), ap(a)), rd(a), rd(out))

    def fill(out, c):
        do("v", lambda: g.vector.memset(ap(out), c), [], rd(out))

    def act(out, a, f, bias=0.0, scale=1.0, accum=None):
        if accum is None:
            do("s", lambda: g.scalar.activation(ap(out), ap(a), f, bias=ap(bias), scale=ap(scale)), rd(a, bias, scale), rd(out))
        else:
            do("s", lambda: g.scalar.activation(ap(out), ap(a), f, bias=ap(bias), scale=ap(scale), accum_out=ap(accum)), rd(a, bias, scale), rd(out, accum))

    def mm(out, l, r, start, stop):
        do("t", lambda: g.tensor.matmul(ap(out), ap(l), ap(r), start, stop), rd(l, r), rd(out))

    def iota(out, pattern, base, cm, small=True):
        if small:
            do("g", lambda: g.iota(ap(out), pattern, base, cm, allow_small_or_imprecise_dtypes=True), [], rd(out))
        else:
            do("g", lambda: g.iota(ap(out), pattern, base, cm), [], rd(out))

    def load(q, out, src, sem):
        Q[q].dma_start(ap(out), src).then_inc(T.sem[sem], 16)
        note(sem, 16, None, [], rd(out))

    def store(q, dst, src, sem):
        need(q, rd(src), [])
        Q[q].dma_start(dst, ap(src)).then_inc(T.sem[sem], 16)
        note(sem, 16, q, rd(src), [])

    sent = [0]

    def send(src, dst, to, sem):
        c = T.cores[to]
        m = 0
        for e in topo.engines(core, c)[:NENG]:
            m |= 1 << e
        rid, pid, _ = topo.addr(c)
        need("g", rd(src), [])
        g.remote_dma(ap(dst), ap(src), T.sem[sem], T.sem["rl"], pid, rid, m)
        sent[0] += NENG

    load("y", ref("x0"), T.xw[:, :], "lx")
    load("y", ref("wti"), T.wts[:, :], "lw")
    load("s", ref("lx", 0, W), T.lex[:, :], "ll")
    load("y", ref("m0"), T.gw[:, :], "lg")
    load("y", ref("thi"), T.th[:, :], "lt")
    load("s", ref("mn", 0, W), T.mng[:, :], "lm")
    for t in (1, 2, 3):
        note("ax%d" % t, NENG, None, [], [ref("x%d" % t)])
        note("ag%d" % t, NENG, None, [], [ref("m%d" % t)])

    iota(ref("pi"), [[1, 1]], 0, 1, False)
    iota(ref("cq"), [[1, 128]], 0, 0)
    iota(ref("cg"), [[1, 8], [0, 16]], 0, 0)
    iota(ref("cl"), [[0, 8], [1, 16]], 0, 0)
    iota(ref("i64"), [[1, 64]], 0, 0)
    iota(ref("ci"), [[16, 24]], 4096, 0)
    iota(ref("wr3"), [[-100, 16], [1, 8], [100, 16]], 0, 0)
    iota(ref("sbi"), [[16, 4], [0, 8], [1, 16]], 0, 0)

    def col(j):
        return ref("col", j, j + 1)
    PG, PL, PP, PLM, THR, W1, W2, THA, THB, C_FAM, C_FBM, C_WA = 0, 1, 2, 3, 4, 7, 8, 9, 10, 11, 12, 13
    B, Id = ref("B"), ref("Id")
    ts(ref("pj", 0, 1), ref("pi"), 4, A.arith_shift_right)
    ts(ref("pj", 1, 2), ref("pi"), 15, A.bitwise_and)
    fill(ref("C6"), 6144.0)
    fill(ref("one"), 1.0)
    fill(ref("zz"), 0.0)
    fill(ref("neg"), -1.0 / 128)
    cp(col(PG), ref("pj", 0, 1))
    cp(col(PL), ref("pj", 1, 2))
    cp(col(PP), ref("pi"))
    ts(Id, ref("cq"), col(PP), A.is_equal)
    ts(B, ref("cg"), col(PG), A.is_equal)
    act(ref("NI4"), Id, AF.Copy, scale=-4096.0)
    tt(ref("BmI"), B, Id, A.subtract)
    ts(ref("eq"), ref("cl", 0, 16), col(PL), A.is_equal)
    fill(ref("CK"), 0.0)
    ts(ref("cw"), ref("eq"), -17.0, A.mult, 1.0, A.add)
    cp(ref("B8"), ref("B", 0, 128, 16))
    cp(ref("col", W1, W1 + 2), ref("wti"))
    ts(ref("Wa"), ref("BmI"), col(W1), A.mult)
    ts(ref("Wb"), ref("BmI"), col(W2), A.mult)
    for k in range(16):
        ts(ref("CK", 129 * k, 128 * k + 128, 16), ref("B8"), ref("cw", k, k + 1), A.mult)

    def more_constants():
        for name, src, s in (("MI", "Id", -1.0), ("NI16", "Id", -16.0),
                             ("I14", "Id", 2.0 ** -14), ("FLM", "B", 2.0 ** 18), ("B64", "B", 64.0), ("PH", "B8", 0.5), ("MH", "B8", -0.5)):
            act(ref(name), ref(src), AF.Copy, scale=s)
        act(ref("CN"), ref("CK"), AF.Copy, scale=-1.0)

    def picks(mat, scale):
        act(ref(mat), ref("wr3"), AF.Copy, scale=0.0)
        for r in range(16):
            act(ref(mat, 129 * r, 128 * r + 128, 16), ref("B8"), AF.Copy, scale=ref(scale, r, r + 1))

    def v_constants():
        ts(ref("up"), ref("cl"), col(PL), A.is_gt)
        ts(ref("pj", 2, 3), ref("thi"), 4, A.arith_shift_right)
        ts(ref("pj", 3, 4), ref("thi"), 15, A.bitwise_and)
        ts(col(THR), col(PL), 0.0, A.not_equal)
        tt(ref("L"), ref("up"), B, A.mult)
        ts(ref("WR"), ref("wr3"), col(PG), A.is_equal)
        cp(ref("col", THA, THA + 2), ref("pj", 2, 4))
        ts(ref("Lm"), ref("L"), -128.0, A.mult)
        tt(ref("Gm"), ref("BmI"), ref("L"), A.subtract)
        ts(col(PLM), col(PL), -1.0, A.mult, 3072.0, A.add)
        ts(col(C_FAM), col(THA), -16.0, A.mult)
        ts(col(C_FBM), col(THB), -1.0, A.mult)
        tt(ref("Wv0"), ref("Lm"), Id, A.add)
        ts(ref("Gm"), ref("Gm"), 2.0 ** -14, A.mult)
        ts(col(C_WA), col(THA), -16.0, A.mult, 4096.0, A.add)
        ts(ref("FAm"), B, col(C_FAM), A.mult, 64.0, A.mult)
        ts(ref("FBm"), B, col(C_FBM), A.mult, 64.0, A.mult)
        tt(ref("Wv0", 0, 128, 16), ref("Wv0", 0, 128, 16), ref("Gm", 0, 128, 16), A.subtract)
        ts(ref("WFA"), ref("B8"), col(C_WA), A.mult)
        ts(ref("WFB"), ref("B8"), col(C_FBM), A.mult)

    def late_constants():
        for t in range(1, VIS):
            tt(ref("Wv%d" % t), ref("Lm"), Id, A.add)
            ts(col(THR + t), col(PL), float(t), A.not_equal)
        ts(ref("SEL", p=64), ref("sbi", p=64), ref("col", PP, PP + 1, p=64), A.is_equal)
        for t in range(1, VIS):
            w = ref("Wv%d" % t, t, 128, 16)
            tt(w, w, ref("Gm", t, 128, 16), A.subtract)
        ts(ref("cim"), ref("ci"), col(PL), A.add)
        ts(ref("ge"), ref("cl", 0, 16), col(PL), A.is_le, -65536.0, A.mult)

    def full(b, n=K):
        return ref("b%d" % b, 0, n)

    def wrap(out, mat, src, first, last):
        for r in range(16):
            mm(out, ref(mat, 128 * r, 128 * r + 128), ref(src, r, K, 16), first and r == 0, last and r == 15)

    lexw, mngw = ref("lx", 0, W), ref("mn", 0, W)

    def spread(t, b, on_v):
        i0, i1 = BLK[b]
        for k in range(16):
            o, s = ref("X16", 16 * i0 + k, 16 * i1, 16), ref("x%d" % t, i0, i1)
            if on_v:
                cp(o, s)
            else:
                act(o, s, AF.Copy)

    def hash_s(t, b):
        hash_1(t, b)
        hash_2(b)
        hash_3(b)

    def hash_1(t, b):
        i0, i1 = HBL[b]
        n = i1 - i0
        xs = ref("x%d" % t, i0, i1)
        mm(ref("b0", 0, n), ref("Wa"), xs, True, True)
        mm(ref("b0", n, 2 * n), ref("Wb"), xs, True, True)
        mm(full(2, n), ref("Wb"), xs, True, False)
        mm(full(1, n), ref("C6"), ref("one", 0, n), True, False)
        mm(full(1, n), ref("Wa"), xs, False, False)

    def hash_2(b):
        n = HBL[b][1] - HBL[b][0]
        act(ref("Mh", 0, 2 * n), ref("b0", 0, 2 * n), AF.Identity, bias=192.0 - 4095.0 / 8192.0, scale=1.0 / 4096.0)

    def hash_3(b):
        n = HBL[b][1] - HBL[b][0]
        mm(full(2, n), ref("NI4"), ref("Mh", n, 2 * n), False, True)
        mm(full(1, n), ref("NI4"), ref("Mh", 0, n), False, True)
        act(ref("UP", 0, n), full(2, n), AF.Identity, bias=786432.0)

    def hash_v(b):
        i0, i1 = HBL[b]
        n = i1 - i0
        hv = [(0, n // 2), (n // 2, n)]
        for a, e in hv:
            tt(ref("pr", a, e), ref("UP", a, e), ref("b1", a, e), A.mult)
        for a, e in hv:
            ts(ref("ps", a, e), ref("pr", a, e), 5, A.arith_shift_right)
        for a, e in hv:
            tt(ref("pt", a, e), ref("ps", a, e), ref("b1", a, e), A.add)
        for a, e in hv:
            ts(ref("hi", i0 + a, i0 + e), ref("pt", a, e), 4095, A.bitwise_and)
        for a, e in hv:
            cp(ref("hu", i0 + a, i0 + e), ref("hi", i0 + a, i0 + e))

    def pick(i0, i1):
        tt(ref("D", 16 * i0, 16 * i1), ind(lexw, ref("hu", i0, i1)), ref("X16", 16 * i0, 16 * i1), A.not_equal)

    def count(b):
        i0, i1 = BLK[b]
        for k in range(16):
            mm(ref("b3", i0, i1), ref("CK", 128 * k, 128 * k + 128), ref("D", 16 * i0 + k, 16 * i1, 16), k == 0, k == 15)

    def look_s(t, b):
        i0, i1 = BLK[b]
        n = i1 - i0
        w, o = lexw, ref("hu", i0, i1)
        do("s", lambda: g.scalar.activation(ref("C")[3], w[3].indirect(o[3]), AF.Copy), [w, o], [ref("C")])
        for h in range(2):
            for k in range(8):
                c = ref("b%d" % (6 + h), n * k, n * k + n)
                mm(c, ref("MI"), ref("x%d" % t, i0, i1), True, False)
                mm(c, Id, ref("C", 8 * h + k, 1024, 16), False, True)

    def unlike_s():
        for h in range(2):
            act(ref("CA", 512 * h, 512 * h + 512), full(6 + h, 512), AF.Abs)
        act(ref("C"), ref("CA"), AF.Relu, bias=1.0, scale=-1.0)

    def count_s(b):
        i0, i1 = BLK[b]
        n = i1 - i0
        mm(ref("b3", i0, i1), ref("one", 0, 128), ref("neg", 0, n), True, False)
        for h in range(2):
            for k in range(8):
                j = 8 * h + k
                mm(ref("b3", i0, i1), ref("CN", 128 * j, 128 * j + 128), ref("C", n * j, n * j + n), False, j == 15)

    def scatter(buf, src):
        w, o, s = ref(buf), ref("lo"), ref(src)
        do("v", lambda: g.vector.tensor_copy(w[3].indirect(o[3]), s[3]), [o, s], [w])

    hash_s(0, 0)
    spread(0, 0, True)
    hash_v(0)
    for t in range(VIS):
        x, m, last = "x%d" % t, "m%d" % t, t == VIS - 1
        xn, gn = "xn%d" % t, "gn%d" % t
        to = (rank + 2) % N if last else (rank - 1) % N

        hash_s(t, 1)
        i0, i1 = HBL[1]
        n = i1 - i0
        pick(0, 32)
        tt(ref("pr", 0, n), ref("UP", 0, n), full(1, n), A.mult)
        pick(32, 64)
        ts(ref("ps", 0, n), ref("pr", 0, n), 5, A.arith_shift_right)
        pick(64, 96)
        tt(ref("pt", 0, n), ref("ps", 0, n), full(1, n), A.add)
        pick(96, 128)
        ts(ref("hi", i0, i1), ref("pt", 0, n), 4095, A.bitwise_and)
        ts(full(5, i0), ref("hi", 0, i0), -2048.0, A.add)
        cp(ref("hu", i0, i1), ref("hi", i0, i1))
        count(0)
        spread(t, 1, False)
        if t == 0:
            more_constants()
        look_s(t, 3)
        spread(t, 2, False)
        unlike_s()
        act(full(4), ref(x), AF.Copy)
        pick(*BLK[1])
        count(1)
        count_s(3)
        pick(*BLK[2])
        count(2)
        if t == 0:
            v_constants()
            picks("WI", "eq")
        ts(ref("b5", i0, i1), ref("hi", i0, i1), -2048.0, A.add)
        if t > 0:
            scatter("mn", "gn%d" % (t - 1))

        ts(ref("pm"), full(3), -13.5, A.is_le)
        mm(full(0), ref("Wv%d" % t), ref("pm"), True, True)
        halves = [(0, K // 2), (K // 2, K)]
        for a, e in halves:
            ts(ref("Le", a, e), ref("b0", a, e), col(THR + t), A.is_ge)
        act(ref("nb"), full(0), AF.Abs, bias=col(THR + t))
        act(ref("Fm"), full(0), AF.Relu)
        for a, e in halves:
            tt(ref("Lh", a, e), ref("Le", a, e), ref("b5", a, e), A.mult)
        tt(ref("Lx"), ref("Le"), full(4), A.mult)
        wl = ref("b2", 0, 24)
        wrap(wl, "WR", "Lh", True, True)
        mm(full(1), B, ref("Lx"), True, True)
        act(ref("NP"), ref("nb"), AF.Relu, bias=64.0, scale=-2.0 ** 20)
        ts(ref("le"), wl, 2048.0, A.add)
        ts(ref("hw"), wl, -16384.0, A.add)
        act(ref("XB"), full(1), AF.Identity, bias=192.0 - 15.0 / 32.0, scale=1.0 / 16.0)
        wm = ref("b2", 0, 24)
        mm(wm, B, ref("zz", 0, 24), True, False)
        for c in range(3):
            o, fc = ref("b2", 8 * c, 8 * c + 8), ref("Fm", 128 * c, 128 * c + 128)
            mm(o, fc, ref("WFA"), False, False)
            mm(o, fc, ref("WFB"), False, False)
        mm(ref("b3", 0, 48), B, ref("zz"), True, False)
        for c in range(3):
            lxc = ref("Lx", 128 * c, 128 * c + 128)
            mm(ref("b3", 8 * c, 8 * c + 8), lxc, ref("MH"), False, False)
            mm(ref("b3", 24 + 8 * c, 32 + 8 * c), lxc, ref("PH"), False, False)
        mm(full(6), Id, ref("Lx"), True, False)
        mm(full(6), Id, ref("NP"), False, True)
        mm(full(0), Id, ref(x), True, False)
        mm(full(0), ref("MI"), ref("NP"), False, True)

        tt(ref("d"), ind(mngw, ref("le")), ref(m), A.subtract)
        act(ref("ad"), ref("d"), AF.Abs)
        tt(ref("LC"), ind(lexw, ref("le")), ref("Le"), A.mult)
        act(ref("XC"), ref("XB"), AF.Copy, scale=64.0)
        if t == 0:
            late_constants()
        wl2 = ref("b7", 0, 24)
        for c in range(3):
            mm(ref("b2", 8 * c, 8 * c + 8), ref("ad", 128 * c, 128 * c + 128), ref("B8"), False, c == 2)
        for c in range(3):
            lcc = ref("LC", 128 * c, 128 * c + 128)
            mm(ref("b3", 8 * c, 8 * c + 8), lcc, ref("MH"), False, False)
            mm(ref("b3", 24 + 8 * c, 32 + 8 * c), lcc, ref("MH"), False, c == 2)
        act(ref("mc"), ref("b3", 0, 24), AF.Copy)
        act(ref("rc"), ref("b3", 24, 48), AF.Abs)
        ts(ref("hd"), ref("d"), 0.5, A.mult, -0.25, A.add)
        tt(ref("LCm"), ref("LC"), full(6), A.min)
        ts(ref("nf"), ref("b2", 0, 24), 4095.5, A.is_ge)
        wrap(wl2, "WI", "XC", True, False)
        for q in range(24):
            act(ref("ab", 64 * q, 64 * q + 64), ref("i64"), AF.Abs, bias=ref("mc", q, q + 1))

        for q in range(24):
            u = ref("U", 64 * q, 64 * q + 64)
            ts(u, ref("ab", 64 * q, 64 * q + 64), ref("rc", q, q + 1), A.is_equal, ref("nf", q, q + 1), A.mult)
            mm(ref("b1", 0, 64, p=64), u, u, q == 0, q == 23)
            if q == 7:
                mm(full(6), B, ref("Lx"), True, False)
                mm(full(6), ref("NI16"), ref("XB"), False, True)
        act(ref("XT"), full(0), AF.Copy)
        act(ref("la"), full(6), AF.Abs, bias=col(PLM))
        wrap(wl2, "WR", "LC", False, True)
        ts(ref("TS", p=64), ref("b1", 0, 64, p=64), 1.0, A.min)
        ts(ref("lf"), wl2, -12288.0, A.add)
        for b in range(4):
            mm(ref("b2", 64 * b, 64 * b + 64), ref("SEL", 128 * b, 128 * b + 128, p=64), ref("TS", p=64), True, True)
        act(ref("lh"), ref("la"), AF.Relu, bias=1.0, scale=-1.0)
        if t == 0:
            picks("WG", "ge")
        mm(full(3), B, ref("Lh"), True, True)
        for lw, src in (("B64", "Le"), ("FAm", "Fm"), ("FBm", "Fm"), ("B64", "ad")):
            mm(full(5), ref(lw), ref(src), src == "Le", False)
        cp(ref("TW"), ref("b2", 0, 256))
        tt(ref("RF"), ind(ref("TW"), ref("lf")), ref("lh"), A.mult)
        cp(ref("Hb"), full(3))
        mm(full(5), ref("FLM"), ref("RF"), False, True)
        mm(full(4), Id, ref(x), True, False)
        mm(full(4), ref("MI"), ref("Lx"), False, False)
        mm(full(4), Id, ref("LCm"), False, True)
        wl3 = ref("b2", 0, 24)
        mm(full(6), Id, ref(m), True, False)

        ts(ref("M"), full(5), 32.0, A.is_lt, 16384.0, A.mult)
        wrap(wl3, "WI", "M", True, True)
        act(full(1), ref("M"), AF.Copy)
        for a, e in halves:
            tt(ref("tx", a, e), ref("XT", a, e), ref("b5", a, e), A.min)
        for a, e in halves:
            tt(ref(xn, a, e), ref("tx", a, e), ref("b4", a, e), A.max)
        send(ref(xn), ref("x%d" % (t + 1)), to, "ax%d" % (t + 1))
        tt(ref("hp"), ref("hw"), wl3, A.add)
        ts(ref("z3"), wl3, -2.0, A.mult, 34816.0, A.add)
        for q in range(24):
            n, e = K - 16 * q, 384 * q
            ts(ref("E", e, e + n), ref("Hb", 16 * q, K), ref("hp", q, q + 1), A.is_equal)
            mm(ref("b7", 16 * q, K), B, ref("E", e, e + n), q == 0, q == 23)
            if q == 5:
                tt(ref("z3"), ref("z3"), ref("hp"), A.add)
            if q == 8:
                tt(ref("gd"), ref("hd"), full(1), A.mult)
            if q == 11:
                tt(ref("z"), ref("z3"), ref("cim"), A.min)
        act(ref("LB"), full(7), AF.Copy, scale=65536.0)
        wl4 = ref("b5", 0, 24)
        for r in range(16):
            mm(wl4, ref("WG", 128 * r, 128 * r + 128), ref("E", r, 24 * K, K), r == 0, False)
        wrap(wl4, "WI", "LB", False, True)
        mm(full(6), ref("I14"), ref("gd"), False, True)
        act(ref(gn), full(6), AF.Copy)
        send(ref(gn), ref("m%d" % (t + 1)), to, "ag%d" % (t + 1))
        if not last:
            hash_s(t + 1, 0)
            spread(t + 1, 0, False)
        tt(ref("z1"), ref("cim"), wl4, A.min)
        tt(ref("z2"), ref("z1"), ref("z"), A.max)
        cp(ref("lo"), ref("z2"))
        scatter("lx", xn)
        if last:
            store("y", T.yl[:, :], lexw, "ol")
            scatter("mn", gn)
        else:
            hash_v(0)

    half = W // 2
    act(ref("D", 0, half), ref("mn", 0, half), AF.Copy, accum=ref("ya"))
    do("v", lambda: g.vector.tensor_reduce(ref("yb")[3], ref("mn", half, W)[3], AxisListType.X, A.add), [ref("mn", half, W)], [ref("yb")])
    tt(ref("ya"), ref("ya"), ref("yb"), A.add)
    store("y", T.yx[:, :], ref("x3"), "ox")
    store("y", T.yg[:, :], ref("m3"), "og")
    store("y", T.ym[:, :], ref("ya"), "om")
    for q in ("v", "s", "t", "g"):
        g.wait_ge(T.sem[own[q]], cnt[q])
    g.wait_ge(T.sem["rl"], sent[0])
    for s in ("ox", "og", "ol", "om"):
        g.wait_ge(T.sem[s], 16)
